import numpy as np
import ml_dtypes


def mxq(x, axis, fmt="e4m3"):
    dtype, down = {"e4m3": (ml_dtypes.float8_e4m3fn, 7), "e5m2": (ml_dtypes.float8_e5m2, 14)}[fmt]
    v = np.moveaxis(np.asarray(x, np.float32).astype(ml_dtypes.bfloat16).astype(np.float64), axis, -1)
    blocks = v.reshape(v.shape[:-1] + (-1, 32))
    amax = np.abs(blocks).max(-1, keepdims=True)
    byte = np.maximum(np.where(amax > 0, np.frexp(amax)[1] - 1 + 127, 0) - down, 1)
    scale = np.exp2(byte - 127.0)
    codes = (blocks / scale).astype(np.float32).astype(dtype).astype(np.float64)
    return np.moveaxis((codes * scale).reshape(v.shape), -1, axis)


WIDE = False


def mx_kscale(k):
    if not WIDE:
        return np.ones(k)
    levels = np.array([10, -10, 5, -5, 0])
    if k % 512:
        return np.exp2(np.random.permutation(np.resize(levels, k // 32))).repeat(32)
    a = np.empty((k // 512, 16))
    for p in range(k // 512):
        a[p, :8] = np.random.permutation(np.resize(levels, 8))
        for g in range(8):
            far = levels[np.abs(levels - a[p, g]) >= 10]
            a[p, g + 8] = far[np.random.randint(len(far))]
    return np.exp2(a.ravel()).repeat(32)


BF16 = ml_dtypes.bfloat16


def bf(x):
    return np.asarray(x, np.float32).astype(BF16)


def f64(x):
    return np.asarray(x).astype(np.float64)


M, N, D, R, F, H = 3, 4096, 512, 1, 512, 256
RF = R * F


def draw0():
    s = mx_kscale(D)
    t = mx_kscale(F)
    return {
        "x": bf(np.random.standard_normal((M, N, D)) * s),
        "w": bf(np.random.standard_normal((M, D, RF)) / np.sqrt(D) / s[:, None]),
        "b": bf(0.5 * np.random.standard_normal((M, RF))),
        "omega": bf((0.5 + 0.1 * np.random.standard_normal((R, F))) * t[None, :]),
        "wo": bf(np.random.standard_normal((F, H)) / np.sqrt(F) / t[:, None]),
        "bo": bf(0.3 * np.random.standard_normal(H)),
    }


def project_modalities(x, w, b):
    h = mxq(x, 2, "e4m3") @ mxq(w, 1, "e4m3")
    return h + b[:, None, :]


def fuse_ranks(h, omega):
    p = h[0] * h[1] * h[2]
    p = p.reshape(p.shape[0], omega.shape[0], omega.shape[1])
    return np.sum(omega[None, :, :] * p, axis=1)


def core(x, w, b, omega, wo, bo):
    h = project_modalities(f64(x), f64(w), f64(b))
    z = fuse_ranks(h, f64(omega))
    y = (mxq(z, 1, "e4m3") @ mxq(f64(wo), 0, "e4m3")) + f64(bo)[None, :]
    return y


def e4m3fn_bytes(y):
    return np.clip(np.asarray(y, np.float64), -448.0, 448.0).astype(np.float32).astype(ml_dtypes.float8_e4m3fn).view(np.uint8)


def e4m3fn_values(b):
    return np.asarray(b, np.uint8).view(ml_dtypes.float8_e4m3fn).astype(np.float64)


def setup_inputs():
    d = draw0()
    x0 = np.asarray(d['x']).astype(np.float64)
    s = (np.max(np.abs(x0), axis=(0, 1), keepdims=True) / 448.0).astype(np.float32)
    out = {}
    for k, v in d.items():
        if k == 'x':
            out['x_bytes'] = e4m3fn_bytes(x0 / s.astype(np.float64))
            out['x_scale'] = s
        else:
            out[k] = v
    return out


def reference(x_bytes, x_scale, w, b, omega, wo, bo):
    return core(e4m3fn_values(x_bytes) * x_scale.astype(np.float64), w, b, omega, wo, bo)

@@ -1,0 +1,341 @@
+from contextlib import ExitStack
+
+import concourse.mybir as mybir
+from concourse.masks import make_identity
+
+F32 = mybir.dt.float32
+BF16 = mybir.dt.bfloat16
+U32 = mybir.dt.uint32
+U8 = mybir.dt.uint8
+E4M3FN = mybir.dt.float8_e4m3fn
+FP8X4 = mybir.dt.float8_e4m3fn_x4
+MULT = mybir.AluOpType.mult
+ADD = mybir.AluOpType.add
+IDENT = mybir.ActivationFunctionType.Identity
+COPY = mybir.ActivationFunctionType.Copy
+
+MODS, TOKENS, D, F, H = 3, 4096, 512, 512, 256
+FLOPS = 2 * MODS * TOKENS * D * F + 2 * TOKENS * F * H
+P = 128
+CHUNKS = [512] * 7 + [256] * 2
+UNITS2 = ((0, 0, "v"), (0, 1, "v"), (1, 0, "v"), (1, 1, "v"), (2, 0, "v"), (2, 1, "v"))
+UNITS1 = ((0, 0, "v"), (1, 0, "v"), (2, 0, "v"))
+UNITSL = ((0, 0, "v"), (1, 0, "v"), (2, 0, "v"))
+GC = 128
+TRB, HSB, HVB, OB = 3, 2, 2, 1
+CAST_LEAD, T_LEAD = 3, 2
+QLAG_S, QLAG_V = 2, 1
+G_OFF = 1
+VLAST = 3
+UB = 3
+QZ_OFF = 3
+
+
+def tile_lowranktrimodalfusion_t_kernel(tc, x_bytes, x_scale, w, b, omega, wo, bo, out):
+    nc = tc.nc
+    with ExitStack() as ctx:
+        keep = ctx.enter_context(tc.tile_pool(name="keep", bufs=1))
+        raw = ctx.enter_context(tc.tile_pool(name="raw", bufs=1))
+        sb = ctx.enter_context(tc.tile_pool(name="sb", bufs=2))
+        ps = ctx.enter_context(tc.psum_pool(name="ps", bufs=1))
+
+        scale = keep.tile([P, 4], F32, name="scale")
+        b_raw = keep.tile([P, MODS, 4], BF16, name="b_raw")
+        om_raw = keep.tile([P, 4], BF16, name="om_raw")
+        b32 = keep.tile([P, MODS, 4], F32, name="b32")
+        om32 = keep.tile([P, 4], F32, name="om32")
+        omb0 = keep.tile([P, 4], F32, name="omb0")
+        bo_t = keep.tile([P, H], BF16, name="bo_t")
+        ident = keep.tile([P, P], F32, name="ident")
+        warm = keep.tile([P, 1], F32, name="warm")
+        w_codes = keep.tile([P, MODS, F], U32, align_bytes=64, name="w_codes")
+        w_scales = keep.tile([P, MODS, F], U8, align_bytes=64, name="w_scales")
+        wo_codes = keep.tile([P, H], U32, align_bytes=64, name="wo_codes")
+        wo_scales = keep.tile([P, H], U8, align_bytes=64, name="wo_scales")
+
+        ops = []
+
+        def at(slot, phase, fn):
+            ops.append((slot, phase, fn))
+
+        units = [UNITS2 if width == 512 else UNITS1 for width in CHUNKS]
+        units[-1] = UNITSL
+        first = []
+        pos = 0
+        for c in range(len(CHUNKS)):
+            first.append(pos)
+            pos += len(units[c])
+        starts = [sum(CHUNKS[:c]) for c in range(len(CHUNKS))]
+        last = len(CHUNKS) - 1
+
+        xb, xw, xp, xg, xq, xs = {}, {}, {}, {}, {}, {}
+        tr, hp, g0, g2, uu, zg, zq, zs, op, ot = {}, {}, {}, {}, {}, {}, {}, {}, {}, {}
+
+        def load_x(c, m):
+            width = CHUNKS[c]
+            jn = width // P
+            t = sb.tile([P, jn * D], U8, tag="xb%d" % m, bufs=3, name="xb")
+            src = x_bytes[m, starts[c] : starts[c] + width, :].rearrange("(p j) k -> p (j k)", j=jn)
+            nc.sync.dma_start(out=t[:], in_=src)
+            xb[c, m] = t
+
+        def cast(c, m, i):
+            t = sb.tile([P, 1024], BF16, tag="xw", bufs=6, name="xw")
+            nc.scalar.copy(t[:], xb[c, m][:, 1024 * i : 1024 * (i + 1)].bitcast(E4M3FN))
+            xw[c, m, i] = t
+
+        def transpose(c, m, i):
+            words = xw[c, m, i][:].bitcast(F32)
+            t = ps.tile([P, 512], F32, tag="tr", bufs=TRB, name="tr")
+            for u in range(2):
+                for j in range(2):
+                    lo = 256 * j + u
+                    nc.tensor.transpose(
+                        t[:, 256 * u + 128 * j : 256 * u + 128 * (j + 1)], words[:, lo : 256 * (j + 1) : 2], ident[:]
+                    )
+            tr[c, m, i] = t
+
+        def grouped(c, m):
+            if (c, m) not in xg:
+                xg[c, m] = sb.tile([P, CHUNKS[c] * 4], BF16, tag="xg", bufs=6, align_bytes=64, name="xg")
+            return xg[c, m]
+
+        def rescale(c, m, i):
+            nc.vector.tensor_tensor(
+                out=grouped(c, m)[:, 1024 * i : 1024 * (i + 1)].rearrange("p (n u e) -> p n u e", u=2, e=2),
+                in0=tr[c, m, i][:].bitcast(BF16).rearrange("p (u n e) -> p n u e", u=2, e=2),
+                in1=scale[:].rearrange("p (u e) -> p u e", u=2).unsqueeze(1).to_broadcast([P, 256, 2, 2]),
+                op=MULT,
+            )
+
+        def rescale_s(c, m, i):
+            t = sb.tile([P, 4, 256], BF16, tag="xp", bufs=3, name="xp")
+            src = tr[c, m, i][:].bitcast(BF16).rearrange("p (u n e) -> p u e n", u=2, e=2)
+            for k in range(4):
+                nc.scalar.activation(out=t[:, k, :], in_=src[:, k // 2, k % 2, :], func=COPY, scale=scale[:, k : k + 1])
+            xp[c, m, i] = t
+
+        def group_x(c, m, i):
+            nc.gpsimd.tensor_scalar(
+                out=grouped(c, m)[:, 1024 * i : 1024 * (i + 1)].rearrange("p (n t) -> p n t", t=4),
+                in0=xp[c, m, i][:].rearrange("p t n -> p n t"),
+                scalar1=1.0, scalar2=0.0, op0=MULT, op1=ADD,
+            )
+
+        def quant_x(c, m):
+            width = CHUNKS[c]
+            q = sb.tile([P, width], U32, tag="xq%d" % m, bufs=4, align_bytes=64, name="xq")
+            s = sb.tile([P, width], U8, tag="xs%d" % m, bufs=4, align_bytes=64, name="xs")
+            nc.vector.quantize_mx(out=q[:].bitcast(FP8X4), scales=s[:], in_=xg[c, m][:])
+            xq[c, m], xs[c, m] = q, s
+
+        def project(c, t, m):
+            width = CHUNKS[c]
+            tag, bufs = ("hv", HVB) if m == 1 else ("hs", HSB)
+            acc = ps.tile([P, 512], F32, tag=tag, bufs=bufs, name="acc")
+            cols = slice(P * t, P * (t + 1))
+            nc.tensor.matmul_mx(
+                out=acc[:, :width],
+                lhsT=w_codes[:, m, cols].bitcast(FP8X4),
+                lhsT_scale=w_scales[:, m, cols],
+                rhs=xq[c, m][:].bitcast(FP8X4),
+                rhs_scale=xs[c, m][:],
+                start=True,
+                stop=True,
+            )
+            hp[c, t, m] = acc
+
+        def exit0(c, t):
+            width = CHUNKS[c]
+            if t == 0:
+                g0[c] = sb.tile([P, 4, width], F32, tag="g0", bufs=2, name="g0")
+            nc.scalar.activation(
+                out=g0[c][:, t, :], in_=hp[c, t, 0][:, :width], func=IDENT, scale=om32[:, t : t + 1], bias=omb0[:, t : t + 1]
+            )
+
+        def exit2(c, t):
+            width = CHUNKS[c]
+            if t == 0:
+                g2[c] = sb.tile([P, 4, width], F32, tag="g2", bufs=UB, name="g2")
+            nc.scalar.activation(out=g2[c][:, t, :], in_=hp[c, t, 2][:, :width], func=IDENT, bias=b32[:, 2, t : t + 1])
+
+        def fuse(c, t):
+            width = CHUNKS[c]
+            if t == 0:
+                uu[c] = sb.tile([P, 4, width], F32, tag="uu", bufs=UB, name="uu")
+            nc.vector.scalar_tensor_tensor(
+                out=uu[c][:, t, :], in0=hp[c, t, 1][:, :width], scalar=b32[:, 1, t : t + 1], in1=g0[c][:, t, :], op0=ADD, op1=MULT
+            )
+
+        def product(c, j):
+            width = CHUNKS[c]
+            if j == 0:
+                zg[c] = sb.tile([P, width * 4], BF16, tag="zg", bufs=2, align_bytes=64, name="zg")
+            for h in range(P // GC):
+                lo = P * j + GC * h
+                cols = slice(lo, lo + GC)
+                eng = nc.vector if c > last - VLAST else nc.gpsimd
+                eng.tensor_tensor(
+                    out=zg[c][:, 4 * lo : 4 * (lo + GC)].rearrange("p (n t) -> p n t", t=4),
+                    in0=uu[c][:, :, cols].rearrange("p t n -> p n t"),
+                    in1=g2[c][:, :, cols].rearrange("p t n -> p n t"),
+                    op=MULT,
+                )
+
+        def quant_z(c, i):
+            width = CHUNKS[c]
+            if i == 0:
+                zq[c] = sb.tile([P, width], U32, tag="zq", bufs=2, align_bytes=64, name="zq")
+                zs[c] = sb.tile([P, width], U8, tag="zs", bufs=2, align_bytes=64, name="zs")
+            nc.vector.quantize_mx(out=zq[c][:].bitcast(FP8X4), scales=zs[c][:], in_=zg[c][:])
+
+        def project_out(c, i):
+            acc = ps.tile([P, 2, H], F32, tag="o", bufs=OB, name="oacc")
+            for k in range(2):
+                cols = slice(P * (2 * i + k), P * (2 * i + k + 1))
+                nc.tensor.matmul_mx(
+                    out=acc[:, k, :],
+                    lhsT=zq[c][:, cols].bitcast(FP8X4),
+                    lhsT_scale=zs[c][:, cols],
+                    rhs=wo_codes[:].bitcast(FP8X4),
+                    rhs_scale=wo_scales[:],
+                    start=True,
+                    stop=True,
+                )
+            op[c, i] = acc
+
+        def exit_out(c, i):
+            jn = CHUNKS[c] // P
+            if i == 0:
+                ot[c] = sb.tile([P, jn, H], F32, tag="ot", bufs=3, name="ot")
+            nc.vector.tensor_tensor(
+                out=ot[c][:, 2 * i : 2 * i + 2, :],
+                in0=op[c, i][:],
+                in1=bo_t[:].unsqueeze(1).to_broadcast([P, 2, H]),
+                op=ADD,
+            )
+
+        def store(c):
+            width = CHUNKS[c]
+            jn = width // P
+            dst = out[starts[c] : starts[c] + width, :].rearrange("(p j) h -> p (j h)", j=jn)
+            nc.sync.dma_start(out=dst, in_=ot[c][:].rearrange("p j h -> p (j h)"))
+
+        w_raw, w_grp = {}, {}
+
+        def load_w(m):
+            t = raw.tile([P, 4, F], BF16, name="w_raw%d" % m)
+            nc.sync.dma_start(out=t[:], in_=w[m].rearrange("(p j) f -> p j f", j=4))
+            w_raw[m] = t
+
+        def group_w(m, eng):
+            t = raw.tile([P, F * 4], BF16, align_bytes=64, name="w_grp%d" % m)
+            dst = t[:].rearrange("p (t c j) -> p t c j", t=4, j=4)
+            src = w_raw[m][:].rearrange("p j (c t) -> p t c j", t=4)
+            if eng == "v":
+                nc.vector.tensor_copy(out=dst, in_=src)
+            else:
+                for t4 in range(4):
+                    nc.gpsimd.tensor_scalar(out=dst[:, t4], in0=src[:, t4], scalar1=1.0, scalar2=0.0, op0=MULT, op1=ADD)
+            w_grp[m] = t
+
+        def quant_w(m):
+            nc.vector.quantize_mx(out=w_codes[:, m, :].bitcast(FP8X4), scales=w_scales[:, m, :], in_=w_grp[m][:])
+
+        def load_wo():
+            t = raw.tile([P, 4, H], BF16, name="wo_raw")
+            nc.sync.dma_start(out=t[:], in_=wo.rearrange("(p j) h -> p j h", j=4))
+            w_raw["o"] = t
+
+        def group_wo():
+            t = raw.tile([P, H * 4], BF16, align_bytes=64, name="wo_grp")
+            nc.gpsimd.tensor_scalar(
+                out=t[:].rearrange("p (h j) -> p h j", j=4),
+                in0=w_raw["o"][:].rearrange("p j h -> p h j"),
+                scalar1=1.0, scalar2=0.0, op0=MULT, op1=ADD,
+            )
+            w_grp["o"] = t
+
+        def quant_wo():
+            nc.vector.quantize_mx(out=wo_codes[:].bitcast(FP8X4), scales=wo_scales[:], in_=w_grp["o"][:])
+
+        def head():
+            nc.vector.memset(warm[:], 0.0)
+            nc.scalar.dma_start(out=scale[:], in_=x_scale.rearrange("o a (p t) -> p (o a t)", t=4))
+            nc.scalar.dma_start(out=b_raw[:], in_=b.rearrange("m (p t) -> p m t", t=4))
+            nc.scalar.dma_start(out=om_raw[:], in_=omega.rearrange("o (p t) -> p (o t)", t=4))
+            nc.scalar.activation(out=warm[:], in_=warm[:], func=IDENT)
+            make_identity(nc, ident[:])
+            load_x(0, 0)
+            load_w(0)
+            load_x(0, 1)
+            load_w(1)
+            load_x(0, 2)
+            load_w(2)
+            load_wo()
+            nc.sync.dma_start(out=bo_t[:], in_=bo.partition_broadcast(P))
+
+        def constants():
+            nc.vector.tensor_copy(out=b32[:], in_=b_raw[:])
+            nc.vector.tensor_copy(out=om32[:], in_=om_raw[:])
+            nc.vector.tensor_tensor(out=omb0[:], in0=om32[:], in1=b32[:, 0, :], op=MULT)
+
+        at(-9, 0, head)
+        at(-1, 6, lambda: group_w(0, "v"))
+        at(0, 7, lambda: group_w(1, "g"))
+        at(1, 7, lambda: group_w(2, "g"))
+        at(2, 7, group_wo)
+        at(5, 6.5, constants)
+        at(2, 6, lambda: quant_w(0))
+        at(4, 6, lambda: quant_w(1))
+        at(6, 6, lambda: quant_w(2))
+        at(6, 6, quant_wo)
+
+        g_end = 0
+        for c in range(len(CHUNKS)):
+            width = CHUNKS[c]
+            banks = width // 256
+            n = len(units[c])
+            f = first[c]
+            if c > 0:
+                for m in range(MODS):
+                    at(first[c - 1] - 2 + 2 * m, 0, lambda c=c, m=m: load_x(c, m))
+            done = [0] * MODS
+            for idx, (m, i, eng) in enumerate(units[c]):
+                k = f + idx
+                at(k - CAST_LEAD, 1, lambda c=c, m=m, i=i: cast(c, m, i))
+                at(k - T_LEAD, 2, lambda c=c, m=m, i=i: transpose(c, m, i))
+                if eng == "v":
+                    at(k, 5, lambda c=c, m=m, i=i: rescale(c, m, i))
+                    done[m] = max(done[m], k + QLAG_V)
+                else:
+                    at(k - 1, 4, lambda c=c, m=m, i=i: rescale_s(c, m, i))
+                    at(k - 1, 7, lambda c=c, m=m, i=i: group_x(c, m, i))
+                    done[m] = max(done[m], k - 1 + QLAG_S)
+            for m in range(MODS):
+                at(done[m], 6, lambda c=c, m=m: quant_x(c, m))
+            g = max(max(done) + G_OFF, g_end)
+            g_end = g + n
+            for t in range(4):
+                for m in range(MODS):
+                    s = g + (3 * t + m) * n // 12
+                    at(s, 3, lambda c=c, t=t, m=m: project(c, t, m))
+                    if m == 0:
+                        at(s, 4, lambda c=c, t=t: exit0(c, t))
+                    elif m == 1:
+                        at(s + 1, 6, lambda c=c, t=t: fuse(c, t))
+                    else:
+                        at(s, 4, lambda c=c, t=t: exit2(c, t))
+            e = g + n
+            for j in range(width // P):
+                at(e + j, 7, lambda c=c, j=j: product(c, j))
+            q = e + 2 * banks - 2 + QZ_OFF
+            at(q, 6, lambda c=c: quant_z(c, 0))
+            for i in range(banks):
+                at(q + i + 1, 3, lambda c=c, i=i: project_out(c, i))
+                at(q + i + 1, 6, lambda c=c, i=i: exit_out(c, i))
+            at(q + banks, 8, lambda c=c: store(c))
+
+        with tc.manual_schedule():
+            for slot, phase, fn in sorted(ops, key=lambda o: (o[0], o[1])):
+                fn()

@@ -17,18 +17,13 @@ COPY = mybir.ActivationFunctionType.Copy
 MODS, TOKENS, D, F, H = 3, 4096, 512, 512, 256
 FLOPS = 2 * MODS * TOKENS * D * F + 2 * TOKENS * F * H
 P = 128
-CHUNKS = [512] * 7 + [256] * 2
-UNITS2 = ((0, 0, "v"), (0, 1, "v"), (1, 0, "v"), (1, 1, "v"), (2, 0, "v"), (2, 1, "v"))
-UNITS1 = ((0, 0, "v"), (1, 0, "v"), (2, 0, "v"))
-UNITSL = ((0, 0, "v"), (1, 0, "v"), (2, 0, "v"))
+PAIR = 512
+CH = 256
+STEPS = TOKENS // CH
+S_UNITS = tuple(range(1, 16, 2))
 GC = 128
 TRB, HSB, HVB, OB = 3, 2, 2, 1
-CAST_LEAD, T_LEAD = 3, 2
-QLAG_S, QLAG_V = 2, 1
-G_OFF = 1
-VLAST = 3
-UB = 3
-QZ_OFF = 3
+V_TAIL = 2
 
 
 def tile_lowranktrimodalfusion_t_kernel(tc, x_bytes, x_scale, w, b, omega, wo, bo, out):
@@ -53,39 +48,35 @@ def tile_lowranktrimodalfusion_t_kernel(tc, x_bytes, x_scale, w, b, omega, wo, b
         wo_codes = keep.tile([P, H], U32, align_bytes=64, name="wo_codes")
         wo_scales = keep.tile([P, H], U8, align_bytes=64, name="wo_scales")
 
-        ops = []
+        xb, xw, xp, qi, qc, qs = {}, {}, {}, {}, {}, {}
+        tr, hs, hv, g0, g2, uu, op, ot = {}, {}, {}, {}, {}, {}, {}, {}
 
-        def at(slot, phase, fn):
-            ops.append((slot, phase, fn))
-
-        units = [UNITS2 if width == 512 else UNITS1 for width in CHUNKS]
-        units[-1] = UNITSL
-        first = []
-        pos = 0
-        for c in range(len(CHUNKS)):
-            first.append(pos)
-            pos += len(units[c])
-        starts = [sum(CHUNKS[:c]) for c in range(len(CHUNKS))]
-        last = len(CHUNKS) - 1
-
-        xb, xw, xp, xg, xq, xs = {}, {}, {}, {}, {}, {}
-        tr, hp, g0, g2, uu, zg, zq, zs, op, ot = {}, {}, {}, {}, {}, {}, {}, {}, {}, {}
-
-        def load_x(c, m):
-            width = CHUNKS[c]
-            jn = width // P
-            t = sb.tile([P, jn * D], U8, tag="xb%d" % m, bufs=3, name="xb")
-            src = x_bytes[m, starts[c] : starts[c] + width, :].rearrange("(p j) k -> p (j k)", j=jn)
+        def load_x(q, m):
+            t = sb.tile([P, 4 * D], U8, tag="xb%d" % m, bufs=3, name="xb")
+            xb[q, m] = t
+            src = x_bytes[m, PAIR * q : PAIR * (q + 1), :].rearrange("(p j) k -> p (j k)", j=4)
             nc.sync.dma_start(out=t[:], in_=src)
-            xb[c, m] = t
 
-        def cast(c, m, i):
+        def load_x_half(m, h):
+            if h == 0:
+                xb[0, m] = sb.tile([P, 4 * D], U8, tag="xb%d" % m, bufs=3, name="xb")
+            src = x_bytes[m, 0:PAIR, :].rearrange("(p j) k -> p (j k)", j=4)
+            cols = slice(1024 * h, 1024 * (h + 1))
+            nc.sync.dma_start(out=xb[0, m][:, cols], in_=src[:, cols])
+
+        def cast(s, m):
+            if not 0 <= s < STEPS:
+                return
             t = sb.tile([P, 1024], BF16, tag="xw", bufs=6, name="xw")
-            nc.scalar.copy(t[:], xb[c, m][:, 1024 * i : 1024 * (i + 1)].bitcast(E4M3FN))
-            xw[c, m, i] = t
+            lo = 1024 * (s % 2)
+            nc.scalar.copy(t[:], xb[s // 2, m][:, lo : lo + 1024].bitcast(E4M3FN))
+            xw[s, m] = t
 
-        def transpose(c, m, i):
-            words = xw[c, m, i][:].bitcast(F32)
+        def transpose(k):
+            s, m = divmod(k, 3)
+            if s >= STEPS:
+                return
+            words = xw[s, m][:].bitcast(F32)
             t = ps.tile([P, 512], F32, tag="tr", bufs=TRB, name="tr")
             for u in range(2):
                 for j in range(2):
@@ -93,133 +84,132 @@ def tile_lowranktrimodalfusion_t_kernel(tc, x_bytes, x_scale, w, b, omega, wo, b
                     nc.tensor.transpose(
                         t[:, 256 * u + 128 * j : 256 * u + 128 * (j + 1)], words[:, lo : 256 * (j + 1) : 2], ident[:]
                     )
-            tr[c, m, i] = t
+            tr[s, m] = t
 
-        def grouped(c, m):
-            if (c, m) not in xg:
-                xg[c, m] = sb.tile([P, CHUNKS[c] * 4], BF16, tag="xg", bufs=6, align_bytes=64, name="xg")
-            return xg[c, m]
+        def q_in(s):
+            if s not in qi:
+                qi[s] = sb.tile([P, 4096], BF16, tag="qi", bufs=4, align_bytes=64, name="qi")
+            return qi[s]
 
-        def rescale(c, m, i):
+        def is_s(s, m):
+            return m == 0 and s in S_UNITS
+
+        def rescale(s, m):
+            if s >= STEPS or is_s(s, m):
+                return
             nc.vector.tensor_tensor(
-                out=grouped(c, m)[:, 1024 * i : 1024 * (i + 1)].rearrange("p (n u e) -> p n u e", u=2, e=2),
-                in0=tr[c, m, i][:].bitcast(BF16).rearrange("p (u n e) -> p n u e", u=2, e=2),
+                out=q_in(s)[:, 1024 * m : 1024 * (m + 1)].rearrange("p (n u e) -> p n u e", u=2, e=2),
+                in0=tr[s, m][:].bitcast(BF16).rearrange("p (u n e) -> p n u e", u=2, e=2),
                 in1=scale[:].rearrange("p (u e) -> p u e", u=2).unsqueeze(1).to_broadcast([P, 256, 2, 2]),
                 op=MULT,
             )
 
-        def rescale_s(c, m, i):
-            t = sb.tile([P, 4, 256], BF16, tag="xp", bufs=3, name="xp")
-            src = tr[c, m, i][:].bitcast(BF16).rearrange("p (u n e) -> p u e n", u=2, e=2)
+        def rescale_s(s):
+            if not is_s(s, 0):
+                return
+            t = sb.tile([P, 4, 256], BF16, tag="xp", bufs=2, name="xp")
+            src = tr[s, 0][:].bitcast(BF16).rearrange("p (u n e) -> p u e n", u=2, e=2)
             for k in range(4):
                 nc.scalar.activation(out=t[:, k, :], in_=src[:, k // 2, k % 2, :], func=COPY, scale=scale[:, k : k + 1])
-            xp[c, m, i] = t
+            xp[s] = t
 
-        def group_x(c, m, i):
-            nc.gpsimd.tensor_scalar(
-                out=grouped(c, m)[:, 1024 * i : 1024 * (i + 1)].rearrange("p (n t) -> p n t", t=4),
-                in0=xp[c, m, i][:].rearrange("p t n -> p n t"),
-                scalar1=1.0, scalar2=0.0, op0=MULT, op1=ADD,
-            )
+        def group_x(s):
+            if not is_s(s, 0):
+                return
+            nc.scalar.copy(q_in(s)[:, 0:1024].rearrange("p (n t) -> p n t", t=4), xp[s][:].rearrange("p t n -> p n t"))
 
-        def quant_x(c, m):
-            width = CHUNKS[c]
-            q = sb.tile([P, width], U32, tag="xq%d" % m, bufs=4, align_bytes=64, name="xq")
-            s = sb.tile([P, width], U8, tag="xs%d" % m, bufs=4, align_bytes=64, name="xs")
-            nc.vector.quantize_mx(out=q[:].bitcast(FP8X4), scales=s[:], in_=xg[c, m][:])
-            xq[c, m], xs[c, m] = q, s
+        def quant(s, lo, hi):
+            if lo == 0 or s not in qc:
+                qc[s] = sb.tile([P, 1024], U32, tag="qc", bufs=4, align_bytes=64, name="qc")
+                qs[s] = sb.tile([P, 1024], U8, tag="qs", bufs=4, align_bytes=64, name="qs")
+            cols = slice(lo // 4, hi // 4)
+            nc.vector.quantize_mx(out=qc[s][:, cols].bitcast(FP8X4), scales=qs[s][:, cols], in_=q_in(s)[:, lo:hi])
 
-        def project(c, t, m):
-            width = CHUNKS[c]
-            tag, bufs = ("hv", HVB) if m == 1 else ("hs", HSB)
-            acc = ps.tile([P, 512], F32, tag=tag, bufs=bufs, name="acc")
+        def project(s, t, m):
+            if not 0 <= s < STEPS:
+                return
+            if m == 1:
+                if t % 2 == 0:
+                    hv[s, t // 2] = ps.tile([P, 2, CH], F32, tag="hv", bufs=HVB, name="hv")
+                acc = hv[s, t // 2][:, t % 2, :]
+            else:
+                if m == 0:
+                    hs[s, t] = ps.tile([P, 2, CH], F32, tag="hs", bufs=HSB, name="hs")
+                acc = hs[s, t][:, m // 2, :]
             cols = slice(P * t, P * (t + 1))
+            xc = slice(CH * m, CH * (m + 1))
             nc.tensor.matmul_mx(
-                out=acc[:, :width],
+                out=acc,
                 lhsT=w_codes[:, m, cols].bitcast(FP8X4),
                 lhsT_scale=w_scales[:, m, cols],
-                rhs=xq[c, m][:].bitcast(FP8X4),
-                rhs_scale=xs[c, m][:],
+                rhs=qc[s][:, xc].bitcast(FP8X4),
+                rhs_scale=qs[s][:, xc],
                 start=True,
                 stop=True,
             )
-            hp[c, t, m] = acc
 
-        def exit0(c, t):
-            width = CHUNKS[c]
+        def exits(s, t):
+            if not 0 <= s < STEPS:
+                return
             if t == 0:
-                g0[c] = sb.tile([P, 4, width], F32, tag="g0", bufs=2, name="g0")
-            nc.scalar.activation(
-                out=g0[c][:, t, :], in_=hp[c, t, 0][:, :width], func=IDENT, scale=om32[:, t : t + 1], bias=omb0[:, t : t + 1]
-            )
+                g0[s] = sb.tile([P, 4, CH], F32, tag="g0", bufs=3, name="g0")
+                g2[s] = sb.tile([P, 4, CH], F32, tag="g2", bufs=4, name="g2")
+            col = slice(t, t + 1)
+            nc.scalar.activation(out=g0[s][:, t, :], in_=hs[s, t][:, 0, :], func=IDENT, scale=om32[:, col], bias=omb0[:, col])
+            nc.scalar.activation(out=g2[s][:, t, :], in_=hs[s, t][:, 1, :], func=IDENT, bias=b32[:, 2, col])
 
-        def exit2(c, t):
-            width = CHUNKS[c]
+        def fuse(s, t):
+            if not 0 <= s < STEPS:
+                return
             if t == 0:
-                g2[c] = sb.tile([P, 4, width], F32, tag="g2", bufs=UB, name="g2")
-            nc.scalar.activation(out=g2[c][:, t, :], in_=hp[c, t, 2][:, :width], func=IDENT, bias=b32[:, 2, t : t + 1])
-
-        def fuse(c, t):
-            width = CHUNKS[c]
-            if t == 0:
-                uu[c] = sb.tile([P, 4, width], F32, tag="uu", bufs=UB, name="uu")
+                uu[s] = sb.tile([P, 4, CH], F32, tag="uu", bufs=3, name="uu")
             nc.vector.scalar_tensor_tensor(
-                out=uu[c][:, t, :], in0=hp[c, t, 1][:, :width], scalar=b32[:, 1, t : t + 1], in1=g0[c][:, t, :], op0=ADD, op1=MULT
+                out=uu[s][:, t, :], in0=hv[s, t // 2][:, t % 2, :], scalar=b32[:, 1, t : t + 1], in1=g0[s][:, t, :], op0=ADD, op1=MULT
             )
 
-        def product(c, j):
-            width = CHUNKS[c]
-            if j == 0:
-                zg[c] = sb.tile([P, width * 4], BF16, tag="zg", bufs=2, align_bytes=64, name="zg")
-            for h in range(P // GC):
-                lo = P * j + GC * h
-                cols = slice(lo, lo + GC)
-                eng = nc.vector if c > last - VLAST else nc.gpsimd
+        def product(s):
+            if not 0 <= s < STEPS:
+                return
+            eng, width = (nc.vector, CH) if s >= STEPS - V_TAIL else (nc.gpsimd, GC)
+            for lo in range(0, CH, width):
                 eng.tensor_tensor(
-                    out=zg[c][:, 4 * lo : 4 * (lo + GC)].rearrange("p (n t) -> p n t", t=4),
-                    in0=uu[c][:, :, cols].rearrange("p t n -> p n t"),
-                    in1=g2[c][:, :, cols].rearrange("p t n -> p n t"),
+                    out=q_in(s + 2)[:, 3072 + 4 * lo : 3072 + 4 * (lo + width)].rearrange("p (n t) -> p n t", t=4),
+                    in0=uu[s][:, :, lo : lo + width].rearrange("p t n -> p n t"),
+                    in1=g2[s][:, :, lo : lo + width].rearrange("p t n -> p n t"),
                     op=MULT,
                 )
 
-        def quant_z(c, i):
-            width = CHUNKS[c]
-            if i == 0:
-                zq[c] = sb.tile([P, width], U32, tag="zq", bufs=2, align_bytes=64, name="zq")
-                zs[c] = sb.tile([P, width], U8, tag="zs", bufs=2, align_bytes=64, name="zs")
-            nc.vector.quantize_mx(out=zq[c][:].bitcast(FP8X4), scales=zs[c][:], in_=zg[c][:])
-
-        def project_out(c, i):
+        def project_out(s):
+            if not 0 <= s < STEPS:
+                return
             acc = ps.tile([P, 2, H], F32, tag="o", bufs=OB, name="oacc")
             for k in range(2):
-                cols = slice(P * (2 * i + k), P * (2 * i + k + 1))
+                cols = slice(768 + P * k, 768 + P * (k + 1))
                 nc.tensor.matmul_mx(
                     out=acc[:, k, :],
-                    lhsT=zq[c][:, cols].bitcast(FP8X4),
-                    lhsT_scale=zs[c][:, cols],
+                    lhsT=qc[s + 2][:, cols].bitcast(FP8X4),
+                    lhsT_scale=qs[s + 2][:, cols],
                     rhs=wo_codes[:].bitcast(FP8X4),
                     rhs_scale=wo_scales[:],
                     start=True,
                     stop=True,
                 )
-            op[c, i] = acc
+            op[s] = acc
 
-        def exit_out(c, i):
-            jn = CHUNKS[c] // P
-            if i == 0:
-                ot[c] = sb.tile([P, jn, H], F32, tag="ot", bufs=3, name="ot")
+        def exit_out(s):
+            if not 0 <= s < STEPS:
+                return
+            ot[s] = sb.tile([P, 2, H], F32, tag="ot", bufs=3, name="ot")
             nc.vector.tensor_tensor(
-                out=ot[c][:, 2 * i : 2 * i + 2, :],
-                in0=op[c, i][:],
-                in1=bo_t[:].unsqueeze(1).to_broadcast([P, 2, H]),
-                op=ADD,
+                out=ot[s][:], in0=op[s][:], in1=bo_t[:].unsqueeze(1).to_broadcast([P, 2, H]), op=ADD
             )
 
-        def store(c):
-            width = CHUNKS[c]
-            jn = width // P
-            dst = out[starts[c] : starts[c] + width, :].rearrange("(p j) h -> p (j h)", j=jn)
-            nc.sync.dma_start(out=dst, in_=ot[c][:].rearrange("p j h -> p (j h)"))
+        def store(s):
+            if not 0 <= s < STEPS:
+                return
+            q, h = divmod(s, 2)
+            dst = out[PAIR * q : PAIR * (q + 1), :].rearrange("(p j) h -> p j h", j=4)
+            nc.sync.dma_start(out=dst[:, 2 * h : 2 * h + 2, :], in_=ot[s][:])
 
         w_raw, w_grp = {}, {}
 
@@ -234,6 +224,8 @@ def tile_lowranktrimodalfusion_t_kernel(tc, x_bytes, x_scale, w, b, omega, wo, b
             src = w_raw[m][:].rearrange("p j (c t) -> p t c j", t=4)
             if eng == "v":
                 nc.vector.tensor_copy(out=dst, in_=src)
+            elif eng == "s":
+                nc.scalar.copy(dst, src)
             else:
                 for t4 in range(4):
                     nc.gpsimd.tensor_scalar(out=dst[:, t4], in0=src[:, t4], scalar1=1.0, scalar2=0.0, op0=MULT, op1=ADD)
@@ -259,83 +251,95 @@ def tile_lowranktrimodalfusion_t_kernel(tc, x_bytes, x_scale, w, b, omega, wo, b
         def quant_wo():
             nc.vector.quantize_mx(out=wo_codes[:].bitcast(FP8X4), scales=wo_scales[:], in_=w_grp["o"][:])
 
-        def head():
-            nc.vector.memset(warm[:], 0.0)
-            nc.scalar.dma_start(out=scale[:], in_=x_scale.rearrange("o a (p t) -> p (o a t)", t=4))
-            nc.scalar.dma_start(out=b_raw[:], in_=b.rearrange("m (p t) -> p m t", t=4))
-            nc.scalar.dma_start(out=om_raw[:], in_=omega.rearrange("o (p t) -> p (o t)", t=4))
-            nc.scalar.activation(out=warm[:], in_=warm[:], func=IDENT)
-            make_identity(nc, ident[:])
-            load_x(0, 0)
-            load_w(0)
-            load_x(0, 1)
-            load_w(1)
-            load_x(0, 2)
-            load_w(2)
-            load_wo()
-            nc.sync.dma_start(out=bo_t[:], in_=bo.partition_broadcast(P))
-
         def constants():
             nc.vector.tensor_copy(out=b32[:], in_=b_raw[:])
             nc.vector.tensor_copy(out=om32[:], in_=om_raw[:])
             nc.vector.tensor_tensor(out=omb0[:], in0=om32[:], in1=b32[:, 0, :], op=MULT)
 
-        at(-9, 0, head)
-        at(-1, 6, lambda: group_w(0, "v"))
-        at(0, 7, lambda: group_w(1, "g"))
-        at(1, 7, lambda: group_w(2, "g"))
-        at(2, 7, group_wo)
-        at(5, 6.5, constants)
-        at(2, 6, lambda: quant_w(0))
-        at(4, 6, lambda: quant_w(1))
-        at(6, 6, lambda: quant_w(2))
-        at(6, 6, quant_wo)
-
-        g_end = 0
-        for c in range(len(CHUNKS)):
-            width = CHUNKS[c]
-            banks = width // 256
-            n = len(units[c])
-            f = first[c]
-            if c > 0:
-                for m in range(MODS):
-                    at(first[c - 1] - 2 + 2 * m, 0, lambda c=c, m=m: load_x(c, m))
-            done = [0] * MODS
-            for idx, (m, i, eng) in enumerate(units[c]):
-                k = f + idx
-                at(k - CAST_LEAD, 1, lambda c=c, m=m, i=i: cast(c, m, i))
-                at(k - T_LEAD, 2, lambda c=c, m=m, i=i: transpose(c, m, i))
-                if eng == "v":
-                    at(k, 5, lambda c=c, m=m, i=i: rescale(c, m, i))
-                    done[m] = max(done[m], k + QLAG_V)
-                else:
-                    at(k - 1, 4, lambda c=c, m=m, i=i: rescale_s(c, m, i))
-                    at(k - 1, 7, lambda c=c, m=m, i=i: group_x(c, m, i))
-                    done[m] = max(done[m], k - 1 + QLAG_S)
-            for m in range(MODS):
-                at(done[m], 6, lambda c=c, m=m: quant_x(c, m))
-            g = max(max(done) + G_OFF, g_end)
-            g_end = g + n
-            for t in range(4):
-                for m in range(MODS):
-                    s = g + (3 * t + m) * n // 12
-                    at(s, 3, lambda c=c, t=t, m=m: project(c, t, m))
-                    if m == 0:
-                        at(s, 4, lambda c=c, t=t: exit0(c, t))
-                    elif m == 1:
-                        at(s + 1, 6, lambda c=c, t=t: fuse(c, t))
-                    else:
-                        at(s, 4, lambda c=c, t=t: exit2(c, t))
-            e = g + n
-            for j in range(width // P):
-                at(e + j, 7, lambda c=c, j=j: product(c, j))
-            q = e + 2 * banks - 2 + QZ_OFF
-            at(q, 6, lambda c=c: quant_z(c, 0))
-            for i in range(banks):
-                at(q + i + 1, 3, lambda c=c, i=i: project_out(c, i))
-                at(q + i + 1, 6, lambda c=c, i=i: exit_out(c, i))
-            at(q + banks, 8, lambda c=c: store(c))
-
         with tc.manual_schedule():
-            for slot, phase, fn in sorted(ops, key=lambda o: (o[0], o[1])):
-                fn()
+            nc.vector.memset(warm[:], 0.0)
+            load_x_half(0, 0)
+            load_w(0)
+            load_x_half(1, 0)
+            load_x_half(2, 0)
+            load_w(1)
+            load_w(2)
+            for m in range(MODS):
+                load_x_half(m, 1)
+            load_wo()
+            for m in range(MODS):
+                load_x(1, m)
+            nc.sync.dma_start(out=bo_t[:], in_=bo.partition_broadcast(P))
+            nc.scalar.dma_start(out=scale[:], in_=x_scale.rearrange("o a (p t) -> p (o a t)", t=4))
+            nc.scalar.activation(out=warm[:], in_=warm[:], func=IDENT)
+            nc.scalar.dma_start(out=b_raw[:], in_=b.rearrange("m (p t) -> p m t", t=4))
+            nc.scalar.dma_start(out=om_raw[:], in_=omega.rearrange("o (p t) -> p (o t)", t=4))
+            make_identity(nc, ident[:])
+            for m in range(MODS):
+                cast(0, m)
+            group_w(0, "v")
+            transpose(0)
+            transpose(1)
+            group_w(1, "g")
+            for s in range(STEPS + 2):
+                if s % 2 == 0:
+                    for m in range(MODS):
+                        if 4 <= s + 4 < STEPS:
+                            load_x(s // 2 + 2, m)
+                for t, m in ((0, 0), (0, 2), (0, 1), (1, 1)):
+                    project(s - 1, t, m)
+                exits(s - 1, 0)
+                fuse(s - 2, 3)
+                product(s - 2)
+                transpose(3 * s + 2)
+                cast(s + 1, 0)
+                if s == 0:
+                    group_w(2, "s")
+                    group_wo()
+                rescale(s, 0)
+                group_x(s)
+                fuse(s - 1, 0)
+                project(s - 1, 1, 0)
+                project(s - 1, 1, 2)
+                exits(s - 1, 1)
+                project_out(s - 3)
+                transpose(3 * s + 3) if not (s + 1 >= STEPS) else None
+                project(s - 1, 2, 0)
+                project(s - 1, 2, 2)
+                cast(s + 1, 1)
+                exits(s - 1, 2)
+                rescale(s, 1)
+                exit_out(s - 3)
+                store(s - 3)
+                fuse(s - 1, 1)
+                if s == 0:
+                    quant_w(0)
+                for t, m in ((2, 1), (3, 1), (3, 0), (3, 2)):
+                    project(s - 1, t, m)
+                transpose(3 * s + 4) if not (s + 1 >= STEPS) else None
+                exits(s - 1, 3)
+                cast(s + 1, 2)
+                rescale_s(s + 1) if s + 1 < STEPS else None
+                rescale(s, 2)
+                fuse(s - 1, 2)
+                if s < 2:
+                    if s == 0:
+                        quant_w(1)
+                        constants()
+                    quant(s, 0, 2048)
+                    quant(s, 2048, 3072)
+                    if s == 0:
+                        quant_w(2)
+                        quant_wo()
+                elif s < STEPS:
+                    quant(s, 0, 4096)
+                elif s == STEPS:
+                    quant(s, 3072, 4096)
+                else:
+                    quant(s, 3072, 4096)
+            project_out(STEPS - 2)
+            project_out(STEPS - 1)
+            exit_out(STEPS - 2)
+            store(STEPS - 2)
+            exit_out(STEPS - 1)
+            store(STEPS - 1)

@@ -20,7 +20,9 @@ P = 128
 PAIR = 512
 CH = 256
 STEPS = TOKENS // CH
-S_UNITS = tuple(range(1, 16, 2))
+S_STEPS = ()
+SINT = "s"
+DUMMY = (1, 1, 1)
 GC = 128
 TRB, HSB, HVB, OB = 3, 2, 2, 1
 V_TAIL = 2
@@ -92,7 +94,7 @@ def tile_lowranktrimodalfusion_t_kernel(tc, x_bytes, x_scale, w, b, omega, wo, b
             return qi[s]
 
         def is_s(s, m):
-            return m == 0 and s in S_UNITS
+            return m == 0 and s in S_STEPS
 
         def rescale(s, m):
             if s >= STEPS or is_s(s, m):
@@ -116,7 +118,12 @@ def tile_lowranktrimodalfusion_t_kernel(tc, x_bytes, x_scale, w, b, omega, wo, b
         def group_x(s):
             if not is_s(s, 0):
                 return
-            nc.scalar.copy(q_in(s)[:, 0:1024].rearrange("p (n t) -> p n t", t=4), xp[s][:].rearrange("p t n -> p n t"))
+            dst = q_in(s)[:, 0:1024].rearrange("p (c i t) -> p c t i", i=4, t=4)
+            src = xp[s][:].rearrange("p t (c i) -> p c t i", i=4)
+            if SINT == "g":
+                nc.gpsimd.tensor_scalar(out=dst, in0=src, scalar1=1.0, scalar2=0.0, op0=MULT, op1=ADD)
+            else:
+                nc.scalar.copy(dst, src)
 
         def quant(s, lo, hi):
             if lo == 0 or s not in qc:
@@ -173,11 +180,19 @@ def tile_lowranktrimodalfusion_t_kernel(tc, x_bytes, x_scale, w, b, omega, wo, b
             eng, width = (nc.vector, CH) if s >= STEPS - V_TAIL else (nc.gpsimd, GC)
             for lo in range(0, CH, width):
                 eng.tensor_tensor(
-                    out=q_in(s + 2)[:, 3072 + 4 * lo : 3072 + 4 * (lo + width)].rearrange("p (n t) -> p n t", t=4),
-                    in0=uu[s][:, :, lo : lo + width].rearrange("p t n -> p n t"),
-                    in1=g2[s][:, :, lo : lo + width].rearrange("p t n -> p n t"),
+                    out=q_in(s + 2)[:, 3072 + 4 * lo : 3072 + 4 * (lo + width)].rearrange("p (c i t) -> p c t i", i=4, t=4),
+                    in0=uu[s][:, :, lo : lo + width].rearrange("p t (c i) -> p c t i", i=4),
+                    in1=g2[s][:, :, lo : lo + width].rearrange("p t (c i) -> p c t i", i=4),
                     op=MULT,
                 )
+
+        def dummy(s, m, n):
+            if s >= STEPS:
+                return
+            for k in range(n):
+                acc = ps.tile([P, 512], F32, tag="o", bufs=OB, name="oacc")
+                lo = 1024 * m
+                nc.tensor.matmul(acc[:, 0:464], lhsT=q_in(s)[:, lo : lo + P], rhs=q_in(s)[:, lo : lo + 464], start=True, stop=True)
 
         def project_out(s):
             if not 0 <= s < STEPS:
@@ -281,14 +296,16 @@ def tile_lowranktrimodalfusion_t_kernel(tc, x_bytes, x_scale, w, b, omega, wo, b
             transpose(0)
             transpose(1)
             group_w(1, "g")
-            for s in range(STEPS + 2):
-                if s % 2 == 0:
+            for s in range(STEPS + 1):
+                c = s - 1
+                nxt = s + 1 < STEPS
+                if s % 2 == 0 and s + 4 < STEPS:
                     for m in range(MODS):
-                        if 4 <= s + 4 < STEPS:
-                            load_x(s // 2 + 2, m)
+                        load_x(s // 2 + 2, m)
+                first_v = 1 if is_s(s, 0) else 0
                 for t, m in ((0, 0), (0, 2), (0, 1), (1, 1)):
-                    project(s - 1, t, m)
-                exits(s - 1, 0)
+                    project(c, t, m)
+                exits(c, 0)
                 fuse(s - 2, 3)
                 product(s - 2)
                 transpose(3 * s + 2)
@@ -296,32 +313,39 @@ def tile_lowranktrimodalfusion_t_kernel(tc, x_bytes, x_scale, w, b, omega, wo, b
                 if s == 0:
                     group_w(2, "s")
                     group_wo()
-                rescale(s, 0)
+                rescale(s, first_v)
                 group_x(s)
-                fuse(s - 1, 0)
-                project(s - 1, 1, 0)
-                project(s - 1, 1, 2)
-                exits(s - 1, 1)
+                fuse(c, 0)
+                project(c, 1, 0)
+                project(c, 1, 2)
+                exits(c, 1)
                 project_out(s - 3)
-                transpose(3 * s + 3) if not (s + 1 >= STEPS) else None
-                project(s - 1, 2, 0)
-                project(s - 1, 2, 2)
+                if nxt:
+                    transpose(3 * s + 3)
+                project(c, 2, 0)
+                project(c, 2, 2)
                 cast(s + 1, 1)
-                exits(s - 1, 2)
-                rescale(s, 1)
+                exits(c, 2)
+                if not first_v:
+                    rescale(s, 1)
                 exit_out(s - 3)
                 store(s - 3)
-                fuse(s - 1, 1)
+                dummy(s, first_v, DUMMY[0])
+                fuse(c, 1)
                 if s == 0:
                     quant_w(0)
                 for t, m in ((2, 1), (3, 1), (3, 0), (3, 2)):
-                    project(s - 1, t, m)
-                transpose(3 * s + 4) if not (s + 1 >= STEPS) else None
-                exits(s - 1, 3)
+                    project(c, t, m)
+                if nxt:
+                    transpose(3 * s + 4)
+                dummy(s, first_v, DUMMY[1])
+                exits(c, 3)
                 cast(s + 1, 2)
-                rescale_s(s + 1) if s + 1 < STEPS else None
+                if nxt:
+                    rescale_s(s + 1)
                 rescale(s, 2)
-                fuse(s - 1, 2)
+                dummy(s, 2, DUMMY[2])
+                fuse(c, 2)
                 if s < 2:
                     if s == 0:
                         quant_w(1)
@@ -333,13 +357,15 @@ def tile_lowranktrimodalfusion_t_kernel(tc, x_bytes, x_scale, w, b, omega, wo, b
                         quant_wo()
                 elif s < STEPS:
                     quant(s, 0, 4096)
-                elif s == STEPS:
-                    quant(s, 3072, 4096)
                 else:
                     quant(s, 3072, 4096)
-            project_out(STEPS - 2)
-            project_out(STEPS - 1)
-            exit_out(STEPS - 2)
-            store(STEPS - 2)
-            exit_out(STEPS - 1)
-            store(STEPS - 1)
+            last = STEPS - 1
+            fuse(last, 3)
+            product(last)
+            project_out(last - 1)
+            exit_out(last - 1)
+            store(last - 1)
+            quant(STEPS + 1, 3072, 4096)
+            project_out(last)
+            exit_out(last)
+            store(last)

@@ -19,13 +19,19 @@ FLOPS = 2 * MODS * TOKENS * D * F + 2 * TOKENS * F * H
 P = 128
 PAIR = 512
 CH = 256
-STEPS = TOKENS // CH
-S_STEPS = ()
-SINT = "s"
-DUMMY = (1, 1, 1)
+WIDTHS = [512] * 7 + [256] * 2
+STEPS = 9
 GC = 128
-TRB, HSB, HVB, OB = 3, 2, 2, 1
-V_TAIL = 2
+TRB, H0B, H2B, HVB, OB = 3, 1, 1, 2, 1
+OTAG = "h2"
+DN = 128
+HDUM = 6
+WENG = "ggs"
+BODY0 = "E0 C0 T0 C1 E1 T1 E2 T2 D T3 C2 V0 E4 C3 E3 T4 W2 D E5 D C4 V1 C5 Q V3 K V2 T5 D"
+BODY = "C0 M00 U3 O0 M01 A0 X0 T0 M02 E0 D D B0 P0 C1 E1 E2 T1 D O1 P1 D U0 M10 D Y1 E3 T2 C4 M12 B1 A1 T3 D M11 C2 M22 M31 M20 D B2 E4 D T4 A2 E5 U1 D M30 M21 C3 D A3 Q M32 B3 T5 U2 C5"
+BODY7 = "D M00 O0 D U3 A0 C0 P1 D E1 X0 M02 M01 M10 T0 B0 E0 A1 O1 M20 U0 M11 R0 E2 Y1 M12 A2 M21 D M30 B1 D C2 M22 U1 B2 A3 Q U2 M31 T1 M32 B3 D C1 T2"
+BODY8 = "T2 U3 D E0 O0 X0 M00 A0 D E1 D T1 M01 T0 M10 A1 M02 B0 O1 P1 M21 Y1 U0 M12 B1 M20 R0 M11 A2 E2 M22 M30 A3 B2 U2 M32 D M31 B3 U1 Q D"
+BODYT = "U3 D M00 A0 O0 X0 M10 M01 M11 M02 A1 R0 D B0 D O1 X1 D Q D U0 M20 A2 M12 B1 U1 O0' X0' M21 M30 M22 M31 D A3 U2 B2 U3' M32 B3 R0' Q' D D O0'' X0''"
 
 
 def tile_lowranktrimodalfusion_t_kernel(tc, x_bytes, x_scale, w, b, omega, wo, bo, out):
@@ -50,8 +56,13 @@ def tile_lowranktrimodalfusion_t_kernel(tc, x_bytes, x_scale, w, b, omega, wo, b
         wo_codes = keep.tile([P, H], U32, align_bytes=64, name="wo_codes")
         wo_scales = keep.tile([P, H], U8, align_bytes=64, name="wo_scales")
 
+        starts = [sum(WIDTHS[:s]) for s in range(STEPS)]
+        base = [3 * start // 256 for start in starts]
+        place = [(s, m, h) for s in range(STEPS) for m in range(MODS) for h in range(WIDTHS[s] // 256)]
+        widths = WIDTHS + [0, 0]
         xb, xw, xp, qi, qc, qs = {}, {}, {}, {}, {}, {}
-        tr, hs, hv, g0, g2, uu, op, ot = {}, {}, {}, {}, {}, {}, {}, {}
+        tr, hp, g0, g2, uu, op, ot = {}, {}, {}, {}, {}, {}, {}
+        junk = ps.tile([P, 512], F32, tag="junk", bufs=1, name="junk")
 
         def load_x(q, m):
             t = sb.tile([P, 4 * D], U8, tag="xb%d" % m, bufs=3, name="xb")
@@ -66,19 +77,22 @@ def tile_lowranktrimodalfusion_t_kernel(tc, x_bytes, x_scale, w, b, omega, wo, b
             cols = slice(1024 * h, 1024 * (h + 1))
             nc.sync.dma_start(out=xb[0, m][:, cols], in_=src[:, cols])
 
-        def cast(s, m):
-            if not 0 <= s < STEPS:
+        def cast(unit):
+            if unit >= len(place):
                 return
-            t = sb.tile([P, 1024], BF16, tag="xw", bufs=6, name="xw")
-            lo = 1024 * (s % 2)
-            nc.scalar.copy(t[:], xb[s // 2, m][:, lo : lo + 1024].bitcast(E4M3FN))
-            xw[s, m] = t
+            s, m, h = place[unit]
+            pair, h = starts[s] // PAIR, starts[s] % PAIR // 256 + h
+            xw[unit] = sb.tile([P, 1024], BF16, tag="xw", bufs=6, name="xw")
+            src = xb[pair, m][:, 1024 * h : 1024 * (h + 1)].bitcast(E4M3FN)
+            if unit == 0:
+                nc.vector.tensor_copy(out=xw[unit][:], in_=src)
+            else:
+                nc.scalar.copy(xw[unit][:], src)
 
-        def transpose(k):
-            s, m = divmod(k, 3)
-            if s >= STEPS:
+        def transpose(unit):
+            if unit >= len(place):
                 return
-            words = xw[s, m][:].bitcast(F32)
+            words = xw[unit][:].bitcast(F32)
             t = ps.tile([P, 512], F32, tag="tr", bufs=TRB, name="tr")
             for u in range(2):
                 for j in range(2):
@@ -86,145 +100,127 @@ def tile_lowranktrimodalfusion_t_kernel(tc, x_bytes, x_scale, w, b, omega, wo, b
                     nc.tensor.transpose(
                         t[:, 256 * u + 128 * j : 256 * u + 128 * (j + 1)], words[:, lo : 256 * (j + 1) : 2], ident[:]
                     )
-            tr[s, m] = t
+            tr[unit] = t
 
         def q_in(s):
             if s not in qi:
-                qi[s] = sb.tile([P, 4096], BF16, tag="qi", bufs=4, align_bytes=64, name="qi")
+                qi[s] = sb.tile([P, 8192], BF16, tag="qi", bufs=3, align_bytes=64, name="qi")
             return qi[s]
 
-        def is_s(s, m):
-            return m == 0 and s in S_STEPS
-
-        def rescale(s, m):
-            if s >= STEPS or is_s(s, m):
-                return
+        def rescale(unit):
+            s = place[unit][0]
+            lo = 1024 * (unit - base[s])
             nc.vector.tensor_tensor(
-                out=q_in(s)[:, 1024 * m : 1024 * (m + 1)].rearrange("p (n u e) -> p n u e", u=2, e=2),
-                in0=tr[s, m][:].bitcast(BF16).rearrange("p (u n e) -> p n u e", u=2, e=2),
+                out=q_in(s)[:, lo : lo + 1024].rearrange("p (n u e) -> p n u e", u=2, e=2),
+                in0=tr[unit][:].bitcast(BF16).rearrange("p (u n e) -> p n u e", u=2, e=2),
                 in1=scale[:].rearrange("p (u e) -> p u e", u=2).unsqueeze(1).to_broadcast([P, 256, 2, 2]),
                 op=MULT,
             )
 
-        def rescale_s(s):
-            if not is_s(s, 0):
-                return
-            t = sb.tile([P, 4, 256], BF16, tag="xp", bufs=2, name="xp")
-            src = tr[s, 0][:].bitcast(BF16).rearrange("p (u n e) -> p u e n", u=2, e=2)
-            for k in range(4):
-                nc.scalar.activation(out=t[:, k, :], in_=src[:, k // 2, k % 2, :], func=COPY, scale=scale[:, k : k + 1])
-            xp[s] = t
-
-        def group_x(s):
-            if not is_s(s, 0):
-                return
-            dst = q_in(s)[:, 0:1024].rearrange("p (c i t) -> p c t i", i=4, t=4)
-            src = xp[s][:].rearrange("p t (c i) -> p c t i", i=4)
-            if SINT == "g":
-                nc.gpsimd.tensor_scalar(out=dst, in0=src, scalar1=1.0, scalar2=0.0, op0=MULT, op1=ADD)
-            else:
-                nc.scalar.copy(dst, src)
-
         def quant(s, lo, hi):
-            if lo == 0 or s not in qc:
-                qc[s] = sb.tile([P, 1024], U32, tag="qc", bufs=4, align_bytes=64, name="qc")
-                qs[s] = sb.tile([P, 1024], U8, tag="qs", bufs=4, align_bytes=64, name="qs")
-            cols = slice(lo // 4, hi // 4)
-            nc.vector.quantize_mx(out=qc[s][:, cols].bitcast(FP8X4), scales=qs[s][:, cols], in_=q_in(s)[:, lo:hi])
+            if s not in qc:
+                qc[s] = sb.tile([P, 2048], U32, tag="qc", bufs=3, align_bytes=64, name="qc")
+                qs[s] = sb.tile([P, 2048], U8, tag="qs", bufs=3, align_bytes=64, name="qs")
+            while lo < hi:
+                size = min(4096, hi - lo)
+                if size == 3072:
+                    size = 2048
+                cols = slice(lo // 4, (lo + size) // 4)
+                nc.vector.quantize_mx(
+                    out=qc[s][:, cols].bitcast(FP8X4), scales=qs[s][:, cols], in_=q_in(s)[:, lo : lo + size]
+                )
+                lo += size
 
-        def project(s, t, m):
-            if not 0 <= s < STEPS:
+        def project(q, t, m):
+            if q < 0:
                 return
-            if m == 1:
-                if t % 2 == 0:
-                    hv[s, t // 2] = ps.tile([P, 2, CH], F32, tag="hv", bufs=HVB, name="hv")
-                acc = hv[s, t // 2][:, t % 2, :]
-            else:
-                if m == 0:
-                    hs[s, t] = ps.tile([P, 2, CH], F32, tag="hs", bufs=HSB, name="hs")
-                acc = hs[s, t][:, m // 2, :]
+            tag, bufs = (("h0", H0B), ("hv", HVB), ("h2", H2B))[m]
+            acc = ps.tile([P, PAIR], F32, tag=tag, bufs=bufs, name="acc")
             cols = slice(P * t, P * (t + 1))
-            xc = slice(CH * m, CH * (m + 1))
+            xc = slice(widths[q] * m, widths[q] * (m + 1))
+            hp[q, t, m] = acc[:, 0 : widths[q]]
             nc.tensor.matmul_mx(
-                out=acc,
+                out=hp[q, t, m],
                 lhsT=w_codes[:, m, cols].bitcast(FP8X4),
                 lhsT_scale=w_scales[:, m, cols],
-                rhs=qc[s][:, xc].bitcast(FP8X4),
-                rhs_scale=qs[s][:, xc],
+                rhs=qc[q][:, xc].bitcast(FP8X4),
+                rhs_scale=qs[q][:, xc],
                 start=True,
                 stop=True,
             )
 
-        def exits(s, t):
-            if not 0 <= s < STEPS:
+        def exit0(q, t):
+            if q < 0:
                 return
-            if t == 0:
-                g0[s] = sb.tile([P, 4, CH], F32, tag="g0", bufs=3, name="g0")
-                g2[s] = sb.tile([P, 4, CH], F32, tag="g2", bufs=4, name="g2")
+            if q not in g0:
+                g0[q] = sb.tile([P, 4, widths[q]], F32, tag="g0", bufs=2, name="g0")
             col = slice(t, t + 1)
-            nc.scalar.activation(out=g0[s][:, t, :], in_=hs[s, t][:, 0, :], func=IDENT, scale=om32[:, col], bias=omb0[:, col])
-            nc.scalar.activation(out=g2[s][:, t, :], in_=hs[s, t][:, 1, :], func=IDENT, bias=b32[:, 2, col])
+            nc.scalar.activation(out=g0[q][:, t, :], in_=hp[q, t, 0], func=IDENT, scale=om32[:, col], bias=omb0[:, col])
 
-        def fuse(s, t):
-            if not 0 <= s < STEPS:
+        def exit2(q, t):
+            if q < 0:
                 return
-            if t == 0:
-                uu[s] = sb.tile([P, 4, CH], F32, tag="uu", bufs=3, name="uu")
+            if q not in g2:
+                g2[q] = sb.tile([P, 4, widths[q]], F32, tag="g2", bufs=2, name="g2")
+            nc.scalar.activation(out=g2[q][:, t, :], in_=hp[q, t, 2], func=IDENT, bias=b32[:, 2, t : t + 1])
+
+        def fuse(q, t):
+            if q < 0:
+                return
+            if q not in uu:
+                uu[q] = sb.tile([P, 4, widths[q]], F32, tag="uu", bufs=2, name="uu")
             nc.vector.scalar_tensor_tensor(
-                out=uu[s][:, t, :], in0=hv[s, t // 2][:, t % 2, :], scalar=b32[:, 1, t : t + 1], in1=g0[s][:, t, :], op0=ADD, op1=MULT
+                out=uu[q][:, t, :], in0=hp[q, t, 1], scalar=b32[:, 1, t : t + 1], in1=g0[q][:, t, :], op0=ADD, op1=MULT
             )
 
-        def product(s):
-            if not 0 <= s < STEPS:
+        def product(q, lo, hi, engine="g"):
+            if q < 0:
                 return
-            eng, width = (nc.vector, CH) if s >= STEPS - V_TAIL else (nc.gpsimd, GC)
-            for lo in range(0, CH, width):
+            eng, width = (nc.vector, hi - lo) if engine == "v" else (nc.gpsimd, GC)
+            for n in range(lo, hi, width):
+                cols = slice(n, n + width)
                 eng.tensor_tensor(
-                    out=q_in(s + 2)[:, 3072 + 4 * lo : 3072 + 4 * (lo + width)].rearrange("p (c i t) -> p c t i", i=4, t=4),
-                    in0=uu[s][:, :, lo : lo + width].rearrange("p t (c i) -> p c t i", i=4),
-                    in1=g2[s][:, :, lo : lo + width].rearrange("p t (c i) -> p c t i", i=4),
+                    out=q_in(q + 2)[:, 12 * widths[q + 2] + 4 * n : 12 * widths[q + 2] + 4 * (n + width)].rearrange("p (c i t) -> p c t i", i=4, t=4),
+                    in0=uu[q][:, :, cols].rearrange("p t (c i) -> p c t i", i=4),
+                    in1=g2[q][:, :, cols].rearrange("p t (c i) -> p c t i", i=4),
                     op=MULT,
                 )
 
-        def dummy(s, m, n):
-            if s >= STEPS:
-                return
+        def dummy(n):
             for k in range(n):
-                acc = ps.tile([P, 512], F32, tag="o", bufs=OB, name="oacc")
-                lo = 1024 * m
-                nc.tensor.matmul(acc[:, 0:464], lhsT=q_in(s)[:, lo : lo + P], rhs=q_in(s)[:, lo : lo + 464], start=True, stop=True)
+                nc.tensor.matmul(junk[:, 0:DN], lhsT=ident[:], rhs=ident[:, 0:DN], start=True, stop=True)
 
-        def project_out(s):
-            if not 0 <= s < STEPS:
+        def project_out(q, i):
+            if q < 0 or i >= widths[q] // 256:
                 return
-            acc = ps.tile([P, 2, H], F32, tag="o", bufs=OB, name="oacc")
+            acc = ps.tile([P, 2, H], F32, tag=OTAG, bufs=OB, name="oacc")
             for k in range(2):
-                cols = slice(768 + P * k, 768 + P * (k + 1))
+                lo = 3 * widths[q + 2] + P * (2 * i + k)
                 nc.tensor.matmul_mx(
                     out=acc[:, k, :],
-                    lhsT=qc[s + 2][:, cols].bitcast(FP8X4),
-                    lhsT_scale=qs[s + 2][:, cols],
+                    lhsT=qc[q + 2][:, lo : lo + P].bitcast(FP8X4),
+                    lhsT_scale=qs[q + 2][:, lo : lo + P],
                     rhs=wo_codes[:].bitcast(FP8X4),
                     rhs_scale=wo_scales[:],
                     start=True,
                     stop=True,
                 )
-            op[s] = acc
+            op[q, i] = acc
 
-        def exit_out(s):
-            if not 0 <= s < STEPS:
+        def exit_out(q, i, engine):
+            if q < 0 or i >= widths[q] // 256:
                 return
-            ot[s] = sb.tile([P, 2, H], F32, tag="ot", bufs=3, name="ot")
-            nc.vector.tensor_tensor(
-                out=ot[s][:], in0=op[s][:], in1=bo_t[:].unsqueeze(1).to_broadcast([P, 2, H]), op=ADD
-            )
-
-        def store(s):
-            if not 0 <= s < STEPS:
-                return
-            q, h = divmod(s, 2)
-            dst = out[PAIR * q : PAIR * (q + 1), :].rearrange("(p j) h -> p j h", j=4)
-            nc.sync.dma_start(out=dst[:, 2 * h : 2 * h + 2, :], in_=ot[s][:])
+            res = sb.tile([P, 2, H], F32, tag="ot", bufs=4, name="ot")
+            bias = bo_t[:].unsqueeze(1).to_broadcast([P, 2, H])
+            if engine == "v":
+                nc.vector.tensor_tensor(out=res[:], in0=op[q, i][:], in1=bias, op=ADD)
+            else:
+                o_raw = sb.tile([P, 2, H], F32, tag="o_raw", bufs=3, name="o_raw")
+                nc.scalar.copy(o_raw[:], op[q, i][:])
+                nc.gpsimd.tensor_tensor(out=res[:], in0=o_raw[:], in1=bias, op=ADD)
+            pair, j = starts[q] // PAIR, 2 * (starts[q] % PAIR // 256 + i)
+            dst = out[PAIR * pair : PAIR * (pair + 1), :].rearrange("(p j) h -> p j h", j=4)
+            nc.sync.dma_start(out=dst[:, j : j + 2, :], in_=res[:])
 
         w_raw, w_grp = {}, {}
 
@@ -271,16 +267,53 @@ def tile_lowranktrimodalfusion_t_kernel(tc, x_bytes, x_scale, w, b, omega, wo, b
             nc.vector.tensor_copy(out=om32[:], in_=om_raw[:])
             nc.vector.tensor_tensor(out=omb0[:], in0=om32[:], in1=b32[:, 0, :], op=MULT)
 
+        def emit(item, s):
+            kind = item[0]
+            t = int(item[1]) if len(item) > 1 else 0
+            if kind == "U":
+                fuse(s - 1 - (t == 3), t)
+            elif kind in "PR":
+                if s >= 2 and t < widths[s - 2] // 256:
+                    product(s - 2, CH * t, CH * (t + 1), "g" if kind == "P" else "v")
+            elif kind == "M":
+                project(s - 1, t, int(item[2]))
+            elif kind == "A":
+                exit0(s - 1, t)
+            elif kind == "B":
+                exit2(s - 1, t)
+            elif kind == "O":
+                project_out(s - 3, t)
+            elif kind in "XY":
+                exit_out(s - 3, t, "v" if kind == "X" else "s")
+            elif kind == "C":
+                cast(base[s] + 4 + t)
+            elif kind == "E":
+                rescale(base[s] + t)
+            elif kind == "T":
+                transpose(base[s] + 2 + t)
+            elif kind == "D":
+                dummy(1)
+            elif kind == "W":
+                group_w(t, "s")
+            elif kind == "V":
+                if t == 3:
+                    quant_wo()
+                else:
+                    quant_w(t)
+            elif kind == "K":
+                constants()
+            else:
+                quant(s, 0, 12 * widths[s] + (4 * widths[s - 2] if s >= 2 else 0))
+
         with tc.manual_schedule():
             nc.vector.memset(warm[:], 0.0)
             load_x_half(0, 0)
+            load_x_half(0, 1)
             load_w(0)
-            load_x_half(1, 0)
-            load_x_half(2, 0)
+            load_x(0, 1)
             load_w(1)
+            load_x(0, 2)
             load_w(2)
-            for m in range(MODS):
-                load_x_half(m, 1)
             load_wo()
             for m in range(MODS):
                 load_x(1, m)
@@ -290,82 +323,18 @@ def tile_lowranktrimodalfusion_t_kernel(tc, x_bytes, x_scale, w, b, omega, wo, b
             nc.scalar.dma_start(out=b_raw[:], in_=b.rearrange("m (p t) -> p m t", t=4))
             nc.scalar.dma_start(out=om_raw[:], in_=omega.rearrange("o (p t) -> p (o t)", t=4))
             make_identity(nc, ident[:])
-            for m in range(MODS):
-                cast(0, m)
-            group_w(0, "v")
+            dummy(HDUM)
+            for unit in range(4):
+                cast(unit)
             transpose(0)
             transpose(1)
+            group_w(0, "g")
             group_w(1, "g")
+            group_wo()
+            bodies = [BODY0] + [BODY] * 6 + [BODY7, BODY8, BODYT]
             for s in range(STEPS + 1):
-                c = s - 1
-                nxt = s + 1 < STEPS
-                if s % 2 == 0 and s + 4 < STEPS:
+                if s + 2 < TOKENS // PAIR:
                     for m in range(MODS):
-                        load_x(s // 2 + 2, m)
-                first_v = 1 if is_s(s, 0) else 0
-                for t, m in ((0, 0), (0, 2), (0, 1), (1, 1)):
-                    project(c, t, m)
-                exits(c, 0)
-                fuse(s - 2, 3)
-                product(s - 2)
-                transpose(3 * s + 2)
-                cast(s + 1, 0)
-                if s == 0:
-                    group_w(2, "s")
-                    group_wo()
-                rescale(s, first_v)
-                group_x(s)
-                fuse(c, 0)
-                project(c, 1, 0)
-                project(c, 1, 2)
-                exits(c, 1)
-                project_out(s - 3)
-                if nxt:
-                    transpose(3 * s + 3)
-                project(c, 2, 0)
-                project(c, 2, 2)
-                cast(s + 1, 1)
-                exits(c, 2)
-                if not first_v:
-                    rescale(s, 1)
-                exit_out(s - 3)
-                store(s - 3)
-                dummy(s, first_v, DUMMY[0])
-                fuse(c, 1)
-                if s == 0:
-                    quant_w(0)
-                for t, m in ((2, 1), (3, 1), (3, 0), (3, 2)):
-                    project(c, t, m)
-                if nxt:
-                    transpose(3 * s + 4)
-                dummy(s, first_v, DUMMY[1])
-                exits(c, 3)
-                cast(s + 1, 2)
-                if nxt:
-                    rescale_s(s + 1)
-                rescale(s, 2)
-                dummy(s, 2, DUMMY[2])
-                fuse(c, 2)
-                if s < 2:
-                    if s == 0:
-                        quant_w(1)
-                        constants()
-                    quant(s, 0, 2048)
-                    quant(s, 2048, 3072)
-                    if s == 0:
-                        quant_w(2)
-                        quant_wo()
-                elif s < STEPS:
-                    quant(s, 0, 4096)
-                else:
-                    quant(s, 3072, 4096)
-            last = STEPS - 1
-            fuse(last, 3)
-            product(last)
-            project_out(last - 1)
-            exit_out(last - 1)
-            store(last - 1)
-            quant(STEPS + 1, 3072, 4096)
-            project_out(last)
-            exit_out(last)
-            store(last)
+                        load_x(s + 2, m)
+                for item in bodies[s].split():
+                    emit(item.replace("'", ""), s + item.count("'"))

@@ -20,18 +20,22 @@ P = 128
 PAIR = 512
 CH = 256
 WIDTHS = [512] * 7 + [256] * 2
-STEPS = 9
+STEPS = len(WIDTHS)
 GC = 128
-TRB, H0B, H2B, HVB, OB = 3, 1, 1, 2, 1
+TRB, H0B, H2B, HVB, OB = 3, 1, 2, 2, 2
 OTAG = "h2"
+PLAN = "0" + "12" * 3 + "78T"
+QIB, QCB, GB = 3, 3, 2
 DN = 128
+NB = 1
 HDUM = 6
 WENG = "ggs"
-BODY0 = "E0 C0 T0 C1 E1 T1 E2 T2 D T3 C2 V0 E4 C3 E3 T4 W2 D E5 D C4 V1 C5 Q V3 K V2 T5 D"
-BODY = "C0 M00 U3 O0 M01 A0 X0 T0 M02 E0 D D B0 P0 C1 E1 E2 T1 D O1 P1 D U0 M10 D Y1 E3 T2 C4 M12 B1 A1 T3 D M11 C2 M22 M31 M20 D B2 E4 D T4 A2 E5 U1 D M30 M21 C3 D A3 Q M32 B3 T5 U2 C5"
-BODY7 = "D M00 O0 D U3 A0 C0 P1 D E1 X0 M02 M01 M10 T0 B0 E0 A1 O1 M20 U0 M11 R0 E2 Y1 M12 A2 M21 D M30 B1 D C2 M22 U1 B2 A3 Q U2 M31 T1 M32 B3 D C1 T2"
-BODY8 = "T2 U3 D E0 O0 X0 M00 A0 D E1 D T1 M01 T0 M10 A1 M02 B0 O1 P1 M21 Y1 U0 M12 B1 M20 R0 M11 A2 E2 M22 M30 A3 B2 U2 M32 D M31 B3 U1 Q D"
-BODYT = "U3 D M00 A0 O0 X0 M10 M01 M11 M02 A1 R0 D B0 D O1 X1 D Q D U0 M20 A2 M12 B1 U1 O0' X0' M21 M30 M22 M31 D A3 U2 B2 U3' M32 B3 R0' Q' D D O0'' X0''"
+BODY0 = "C0 E0 G0 C1 E1 C3 C2 E2 W2 T2 T3 T1 C4 V0 E4 E5 E3 T4 Q C5 V1 K T5 V2 V3"
+BODY = "C4 U3 O0 M01 M00 E0 G0 T1 M02 X0 E1 C1 C0 A0 E2 O1 M10 E3 B0 G2 U0 M12 P0 E4 P1 G3 Y1 M11 C2 A1 M22 M20 G4 M32 U1 E5 B1 M21 C3 A2 C5 U2 M30 B2 Q A3 M31 G5 B3"
+BODY2 = "T0 M00 M01 C2 U3 C1 A0 M02 E0 O0 M10 C0 G1 G3 M12 A1 E1 O1 B0 X0 P1 Z2 B1 E3 M11 M21 I2 U0 M22 M20 C4 B2 G2 E5 A2 X1 M31 C3 P0 T4 U1 M30 A3 E4 M32 Q C5 U2 T5 B3"
+BODY7 = "U3 O0 M00 M02 M01 X0 M22 M10 G0 E1 A0 C0 M20 M12 A1 M11 E0 U0 E2 R0 O1 B0 B2 P1 M21 C2 B1 A2 M32 T2 G1 Y1 B3 M30 U2 C1 U1 A3 Q M31"
+BODY8 = "O0 M00 M20 U3 P1 M10 M02 A0 M01 E0 M21 T0 X0 M12 R0 O1 A2 B0 M32 M30 B1 T1 M11 A1 Y1 M22 B3 E1 M31 U0 U2 E2 U1 G2 Q A3 B2"
+BODYT = "M00 U3 M11 R0 O0 M02 Q A0 Y0 B0 M01 M10 O0' M20 A1 Y0' O1 M31 U0 M12 M30 U1 M22 M21 A2 X1 U2 B1 M32 A3 B2 U3' B3 R0' Q' O0'' X0''"
 
 
 def tile_lowranktrimodalfusion_t_kernel(tc, x_bytes, x_scale, w, b, omega, wo, bo, out):
@@ -62,7 +66,6 @@ def tile_lowranktrimodalfusion_t_kernel(tc, x_bytes, x_scale, w, b, omega, wo, b
         widths = WIDTHS + [0, 0]
         xb, xw, xp, qi, qc, qs = {}, {}, {}, {}, {}, {}
         tr, hp, g0, g2, uu, op, ot = {}, {}, {}, {}, {}, {}, {}
-        junk = ps.tile([P, 512], F32, tag="junk", bufs=1, name="junk")
 
         def load_x(q, m):
             t = sb.tile([P, 4 * D], U8, tag="xb%d" % m, bufs=3, name="xb")
@@ -89,11 +92,13 @@ def tile_lowranktrimodalfusion_t_kernel(tc, x_bytes, x_scale, w, b, omega, wo, b
             else:
                 nc.scalar.copy(xw[unit][:], src)
 
-        def transpose(unit):
+        def transpose(unit, busy=False):
             if unit >= len(place):
                 return
             words = xw[unit][:].bitcast(F32)
             t = ps.tile([P, 512], F32, tag="tr", bufs=TRB, name="tr")
+            for k in range(NB if busy else 0):
+                nc.tensor.matmul(t[:, 0:DN], lhsT=ident[:], rhs=ident[:, 0:DN], start=True, stop=True)
             for u in range(2):
                 for j in range(2):
                     lo = 256 * j + u
@@ -104,7 +109,7 @@ def tile_lowranktrimodalfusion_t_kernel(tc, x_bytes, x_scale, w, b, omega, wo, b
 
         def q_in(s):
             if s not in qi:
-                qi[s] = sb.tile([P, 8192], BF16, tag="qi", bufs=3, align_bytes=64, name="qi")
+                qi[s] = sb.tile([P, 8192], BF16, tag="qi", bufs=QIB, align_bytes=64, name="qi")
             return qi[s]
 
         def rescale(unit):
@@ -117,10 +122,27 @@ def tile_lowranktrimodalfusion_t_kernel(tc, x_bytes, x_scale, w, b, omega, wo, b
                 op=MULT,
             )
 
+        def rescale_s(unit):
+            t = sb.tile([P, 4, 256], BF16, tag="xp", bufs=2, name="xp")
+            src = tr[unit][:].bitcast(BF16).rearrange("p (u n e) -> p u e n", u=2, e=2)
+            for k in range(4):
+                nc.scalar.activation(out=t[:, k, :], in_=src[:, k // 2, k % 2, :], func=COPY, scale=scale[:, k : k + 1])
+            xp[unit] = t
+
+        def group_x(unit, engine):
+            s = place[unit][0]
+            lo = 1024 * (unit - base[s])
+            dst = q_in(s)[:, lo : lo + 1024].rearrange("p (c i t) -> p c t i", i=4, t=4)
+            src = xp[unit][:].rearrange("p t (c i) -> p c t i", i=4)
+            if engine == "g":
+                nc.gpsimd.tensor_scalar(out=dst, in0=src, scalar1=1.0, scalar2=0.0, op0=MULT, op1=ADD)
+            else:
+                nc.scalar.copy(dst, src)
+
         def quant(s, lo, hi):
             if s not in qc:
-                qc[s] = sb.tile([P, 2048], U32, tag="qc", bufs=3, align_bytes=64, name="qc")
-                qs[s] = sb.tile([P, 2048], U8, tag="qs", bufs=3, align_bytes=64, name="qs")
+                qc[s] = sb.tile([P, 2048], U32, tag="qc", bufs=QCB, align_bytes=64, name="qc")
+                qs[s] = sb.tile([P, 2048], U8, tag="qs", bufs=QCB, align_bytes=64, name="qs")
             while lo < hi:
                 size = min(4096, hi - lo)
                 if size == 3072:
@@ -153,7 +175,7 @@ def tile_lowranktrimodalfusion_t_kernel(tc, x_bytes, x_scale, w, b, omega, wo, b
             if q < 0:
                 return
             if q not in g0:
-                g0[q] = sb.tile([P, 4, widths[q]], F32, tag="g0", bufs=2, name="g0")
+                g0[q] = sb.tile([P, 4, widths[q]], F32, tag="g0", bufs=GB, name="g0")
             col = slice(t, t + 1)
             nc.scalar.activation(out=g0[q][:, t, :], in_=hp[q, t, 0], func=IDENT, scale=om32[:, col], bias=omb0[:, col])
 
@@ -161,14 +183,14 @@ def tile_lowranktrimodalfusion_t_kernel(tc, x_bytes, x_scale, w, b, omega, wo, b
             if q < 0:
                 return
             if q not in g2:
-                g2[q] = sb.tile([P, 4, widths[q]], F32, tag="g2", bufs=2, name="g2")
+                g2[q] = sb.tile([P, 4, widths[q]], F32, tag="g2", bufs=GB, name="g2")
             nc.scalar.activation(out=g2[q][:, t, :], in_=hp[q, t, 2], func=IDENT, bias=b32[:, 2, t : t + 1])
 
         def fuse(q, t):
             if q < 0:
                 return
             if q not in uu:
-                uu[q] = sb.tile([P, 4, widths[q]], F32, tag="uu", bufs=2, name="uu")
+                uu[q] = sb.tile([P, 4, widths[q]], F32, tag="uu", bufs=GB, name="uu")
             nc.vector.scalar_tensor_tensor(
                 out=uu[q][:, t, :], in0=hp[q, t, 1], scalar=b32[:, 1, t : t + 1], in1=g0[q][:, t, :], op0=ADD, op1=MULT
             )
@@ -185,10 +207,6 @@ def tile_lowranktrimodalfusion_t_kernel(tc, x_bytes, x_scale, w, b, omega, wo, b
                     in1=g2[q][:, :, cols].rearrange("p t (c i) -> p c t i", i=4),
                     op=MULT,
                 )
-
-        def dummy(n):
-            for k in range(n):
-                nc.tensor.matmul(junk[:, 0:DN], lhsT=ident[:], rhs=ident[:, 0:DN], start=True, stop=True)
 
         def project_out(q, i):
             if q < 0 or i >= widths[q] // 256:
@@ -289,10 +307,14 @@ def tile_lowranktrimodalfusion_t_kernel(tc, x_bytes, x_scale, w, b, omega, wo, b
                 cast(base[s] + 4 + t)
             elif kind == "E":
                 rescale(base[s] + t)
-            elif kind == "T":
-                transpose(base[s] + 2 + t)
+            elif kind == "Z":
+                rescale_s(base[s] + t)
+            elif kind in "IJ":
+                group_x(base[s] + t, "g" if kind == "J" else "s")
+            elif kind in "TG":
+                transpose(base[s] + 2 + t, kind == "G")
             elif kind == "D":
-                dummy(1)
+                pass
             elif kind == "W":
                 group_w(t, "s")
             elif kind == "V":
@@ -323,7 +345,9 @@ def tile_lowranktrimodalfusion_t_kernel(tc, x_bytes, x_scale, w, b, omega, wo, b
             nc.scalar.dma_start(out=b_raw[:], in_=b.rearrange("m (p t) -> p m t", t=4))
             nc.scalar.dma_start(out=om_raw[:], in_=omega.rearrange("o (p t) -> p (o t)", t=4))
             make_identity(nc, ident[:])
-            dummy(HDUM)
+            warm_ps = ps.tile([P, 512], F32, tag="tr", bufs=TRB, name="warm_ps")
+            for k in range(HDUM):
+                nc.tensor.matmul(warm_ps[:, 0:DN], lhsT=ident[:], rhs=ident[:, 0:DN], start=True, stop=True)
             for unit in range(4):
                 cast(unit)
             transpose(0)
@@ -331,10 +355,10 @@ def tile_lowranktrimodalfusion_t_kernel(tc, x_bytes, x_scale, w, b, omega, wo, b
             group_w(0, "g")
             group_w(1, "g")
             group_wo()
-            bodies = [BODY0] + [BODY] * 6 + [BODY7, BODY8, BODYT]
+            bodies = {"0": BODY0, "1": BODY, "2": BODY2, "7": BODY7, "8": BODY8, "T": BODYT}
             for s in range(STEPS + 1):
-                if s + 2 < TOKENS // PAIR:
+                if s < STEPS and starts[s] % PAIR == 0 and starts[s] // PAIR + 2 < TOKENS // PAIR:
                     for m in range(MODS):
-                        load_x(s + 2, m)
-                for item in bodies[s].split():
+                        load_x(starts[s] // PAIR + 2, m)
+                for item in bodies[PLAN[s]].split():
                     emit(item.replace("'", ""), s + item.count("'"))

from contextlib import ExitStack

import concourse.mybir as mybir
from concourse.masks import make_identity

F32 = mybir.dt.float32
BF16 = mybir.dt.bfloat16
U32 = mybir.dt.uint32
U8 = mybir.dt.uint8
E4M3FN = mybir.dt.float8_e4m3fn
FP8X4 = mybir.dt.float8_e4m3fn_x4
MULT = mybir.AluOpType.mult
ADD = mybir.AluOpType.add
IDENT = mybir.ActivationFunctionType.Identity
COPY = mybir.ActivationFunctionType.Copy

MODS, TOKENS, D, F, H = 3, 4096, 512, 512, 256
FLOPS = 2 * MODS * TOKENS * D * F + 2 * TOKENS * F * H
P = 128
PAIR = 512
CH = 256
WIDTHS = [512] * 7 + [256] * 2
STEPS = len(WIDTHS)
GC = 128
TRB, H0B, H2B, HVB, OB = 3, 1, 2, 2, 2
OTAG = "h2"
PLAN = "0" + "12" * 3 + "78T"
QIB, QCB, GB = 3, 3, 2
DN = 128
NB = 1
HDUM = 6
WENG = "ggs"
BODY0 = "C0 E0 G0 C1 E1 C3 C2 E2 W2 T2 T3 T1 C4 V0 E4 E5 E3 T4 Q C5 V1 K T5 V2 V3"
BODY = "C4 U3 O0 M01 M00 E0 G0 T1 M02 X0 E1 C1 C0 A0 E2 O1 M10 E3 B0 G2 U0 M12 P0 E4 P1 G3 Y1 M11 C2 A1 M22 M20 G4 M32 U1 E5 B1 M21 C3 A2 C5 U2 M30 B2 Q A3 M31 G5 B3"
BODY2 = "T0 M00 M01 C2 U3 C1 A0 M02 E0 O0 M10 C0 G1 G3 M12 A1 E1 O1 B0 X0 P1 Z2 B1 E3 M11 M21 I2 U0 M22 M20 C4 B2 G2 E5 A2 X1 M31 C3 P0 T4 U1 M30 A3 E4 M32 Q C5 U2 T5 B3"
BODY7 = "U3 O0 M00 M02 M01 X0 M22 M10 G0 E1 A0 C0 M20 M12 A1 M11 E0 U0 E2 R0 O1 B0 B2 P1 M21 C2 B1 A2 M32 T2 G1 Y1 B3 M30 U2 C1 U1 A3 Q M31"
BODY8 = "O0 M00 M20 U3 P1 M10 M02 A0 M01 E0 M21 T0 X0 M12 R0 O1 A2 B0 M32 M30 B1 T1 M11 A1 Y1 M22 B3 E1 M31 U0 U2 E2 U1 G2 Q A3 B2"
BODYT = "M00 U3 M11 R0 O0 M02 Q A0 Y0 B0 M01 M10 O0' M20 A1 Y0' O1 M31 U0 M12 M30 U1 M22 M21 A2 X1 U2 B1 M32 A3 B2 U3' B3 R0' Q' O0'' X0''"


def tile_lowranktrimodalfusion_t_kernel(tc, x_bytes, x_scale, w, b, omega, wo, bo, out):
    nc = tc.nc
    with ExitStack() as ctx:
        keep = ctx.enter_context(tc.tile_pool(name="keep", bufs=1))
        raw = ctx.enter_context(tc.tile_pool(name="raw", bufs=1))
        sb = ctx.enter_context(tc.tile_pool(name="sb", bufs=2))
        ps = ctx.enter_context(tc.psum_pool(name="ps", bufs=1))

        scale = keep.tile([P, 4], F32, name="scale")
        b_raw = keep.tile([P, MODS, 4], BF16, name="b_raw")
        om_raw = keep.tile([P, 4], BF16, name="om_raw")
        b32 = keep.tile([P, MODS, 4], F32, name="b32")
        om32 = keep.tile([P, 4], F32, name="om32")
        omb0 = keep.tile([P, 4], F32, name="omb0")
        bo_t = keep.tile([P, H], BF16, name="bo_t")
        ident = keep.tile([P, P], F32, name="ident")
        warm = keep.tile([P, 1], F32, name="warm")
        w_codes = keep.tile([P, MODS, F], U32, align_bytes=64, name="w_codes")
        w_scales = keep.tile([P, MODS, F], U8, align_bytes=64, name="w_scales")
        wo_codes = keep.tile([P, H], U32, align_bytes=64, name="wo_codes")
        wo_scales = keep.tile([P, H], U8, align_bytes=64, name="wo_scales")

        starts = [sum(WIDTHS[:s]) for s in range(STEPS)]
        base = [3 * start // 256 for start in starts]
        place = [(s, m, h) for s in range(STEPS) for m in range(MODS) for h in range(WIDTHS[s] // 256)]
        widths = WIDTHS + [0, 0]
        xb, xw, xp, qi, qc, qs = {}, {}, {}, {}, {}, {}
        tr, hp, g0, g2, uu, op, ot = {}, {}, {}, {}, {}, {}, {}

        def load_x(q, m):
            t = sb.tile([P, 4 * D], U8, tag="xb%d" % m, bufs=3, name="xb")
            xb[q, m] = t
            src = x_bytes[m, PAIR * q : PAIR * (q + 1), :].rearrange("(p j) k -> p (j k)", j=4)
            nc.sync.dma_start(out=t[:], in_=src)

        def load_x_half(m, h):
            if h == 0:
                xb[0, m] = sb.tile([P, 4 * D], U8, tag="xb%d" % m, bufs=3, name="xb")
            src = x_bytes[m, 0:PAIR, :].rearrange("(p j) k -> p (j k)", j=4)
            cols = slice(1024 * h, 1024 * (h + 1))
            nc.sync.dma_start(out=xb[0, m][:, cols], in_=src[:, cols])

        def cast(unit):
            if unit >= len(place):
                return
            s, m, h = place[unit]
            pair, h = starts[s] // PAIR, starts[s] % PAIR // 256 + h
            xw[unit] = sb.tile([P, 1024], BF16, tag="xw", bufs=6, name="xw")
            src = xb[pair, m][:, 1024 * h : 1024 * (h + 1)].bitcast(E4M3FN)
            if unit == 0:
                nc.vector.tensor_copy(out=xw[unit][:], in_=src)
            else:
                nc.scalar.copy(xw[unit][:], src)

        def transpose(unit, busy=False):
            if unit >= len(place):
                return
            words = xw[unit][:].bitcast(F32)
            t = ps.tile([P, 512], F32, tag="tr", bufs=TRB, name="tr")
            for k in range(NB if busy else 0):
                nc.tensor.matmul(t[:, 0:DN], lhsT=ident[:], rhs=ident[:, 0:DN], start=True, stop=True)
            for u in range(2):
                for j in range(2):
                    lo = 256 * j + u
                    nc.tensor.transpose(
                        t[:, 256 * u + 128 * j : 256 * u + 128 * (j + 1)], words[:, lo : 256 * (j + 1) : 2], ident[:]
                    )
            tr[unit] = t

        def q_in(s):
            if s not in qi:
                qi[s] = sb.tile([P, 8192], BF16, tag="qi", bufs=QIB, align_bytes=64, name="qi")
            return qi[s]

        def rescale(unit):
            s = place[unit][0]
            lo = 1024 * (unit - base[s])
            nc.vector.tensor_tensor(
                out=q_in(s)[:, lo : lo + 1024].rearrange("p (n u e) -> p n u e", u=2, e=2),
                in0=tr[unit][:].bitcast(BF16).rearrange("p (u n e) -> p n u e", u=2, e=2),
                in1=scale[:].rearrange("p (u e) -> p u e", u=2).unsqueeze(1).to_broadcast([P, 256, 2, 2]),
                op=MULT,
            )

        def rescale_s(unit):
            t = sb.tile([P, 4, 256], BF16, tag="xp", bufs=2, name="xp")
            src = tr[unit][:].bitcast(BF16).rearrange("p (u n e) -> p u e n", u=2, e=2)
            for k in range(4):
                nc.scalar.activation(out=t[:, k, :], in_=src[:, k // 2, k % 2, :], func=COPY, scale=scale[:, k : k + 1])
            xp[unit] = t

        def group_x(unit, engine):
            s = place[unit][0]
            lo = 1024 * (unit - base[s])
            dst = q_in(s)[:, lo : lo + 1024].rearrange("p (c i t) -> p c t i", i=4, t=4)
            src = xp[unit][:].rearrange("p t (c i) -> p c t i", i=4)
            if engine == "g":
                nc.gpsimd.tensor_scalar(out=dst, in0=src, scalar1=1.0, scalar2=0.0, op0=MULT, op1=ADD)
            else:
                nc.scalar.copy(dst, src)

        def quant(s, lo, hi):
            if s not in qc:
                qc[s] = sb.tile([P, 2048], U32, tag="qc", bufs=QCB, align_bytes=64, name="qc")
                qs[s] = sb.tile([P, 2048], U8, tag="qs", bufs=QCB, align_bytes=64, name="qs")
            while lo < hi:
                size = min(4096, hi - lo)
                if size == 3072:
                    size = 2048
                cols = slice(lo // 4, (lo + size) // 4)
                nc.vector.quantize_mx(
                    out=qc[s][:, cols].bitcast(FP8X4), scales=qs[s][:, cols], in_=q_in(s)[:, lo : lo + size]
                )
                lo += size

        def project(q, t, m):
            if q < 0:
                return
            tag, bufs = (("h0", H0B), ("hv", HVB), ("h2", H2B))[m]
            acc = ps.tile([P, PAIR], F32, tag=tag, bufs=bufs, name="acc")
            cols = slice(P * t, P * (t + 1))
            xc = slice(widths[q] * m, widths[q] * (m + 1))
            hp[q, t, m] = acc[:, 0 : widths[q]]
            nc.tensor.matmul_mx(
                out=hp[q, t, m],
                lhsT=w_codes[:, m, cols].bitcast(FP8X4),
                lhsT_scale=w_scales[:, m, cols],
                rhs=qc[q][:, xc].bitcast(FP8X4),
                rhs_scale=qs[q][:, xc],
                start=True,
                stop=True,
            )

        def exit0(q, t):
            if q < 0:
                return
            if q not in g0:
                g0[q] = sb.tile([P, 4, widths[q]], F32, tag="g0", bufs=GB, name="g0")
            col = slice(t, t + 1)
            nc.scalar.activation(out=g0[q][:, t, :], in_=hp[q, t, 0], func=IDENT, scale=om32[:, col], bias=omb0[:, col])

        def exit2(q, t):
            if q < 0:
                return
            if q not in g2:
                g2[q] = sb.tile([P, 4, widths[q]], F32, tag="g2", bufs=GB, name="g2")
            nc.scalar.activation(out=g2[q][:, t, :], in_=hp[q, t, 2], func=IDENT, bias=b32[:, 2, t : t + 1])

        def fuse(q, t):
            if q < 0:
                return
            if q not in uu:
                uu[q] = sb.tile([P, 4, widths[q]], F32, tag="uu", bufs=GB, name="uu")
            nc.vector.scalar_tensor_tensor(
                out=uu[q][:, t, :], in0=hp[q, t, 1], scalar=b32[:, 1, t : t + 1], in1=g0[q][:, t, :], op0=ADD, op1=MULT
            )

        def product(q, lo, hi, engine="g"):
            if q < 0:
                return
            eng, width = (nc.vector, hi - lo) if engine == "v" else (nc.gpsimd, GC)
            for n in range(lo, hi, width):
                cols = slice(n, n + width)
                eng.tensor_tensor(
                    out=q_in(q + 2)[:, 12 * widths[q + 2] + 4 * n : 12 * widths[q + 2] + 4 * (n + width)].rearrange("p (c i t) -> p c t i", i=4, t=4),
                    in0=uu[q][:, :, cols].rearrange("p t (c i) -> p c t i", i=4),
                    in1=g2[q][:, :, cols].rearrange("p t (c i) -> p c t i", i=4),
                    op=MULT,
                )

        def project_out(q, i):
            if q < 0 or i >= widths[q] // 256:
                return
            acc = ps.tile([P, 2, H], F32, tag=OTAG, bufs=OB, name="oacc")
            for k in range(2):
                lo = 3 * widths[q + 2] + P * (2 * i + k)
                nc.tensor.matmul_mx(
                    out=acc[:, k, :],
                    lhsT=qc[q + 2][:, lo : lo + P].bitcast(FP8X4),
                    lhsT_scale=qs[q + 2][:, lo : lo + P],
                    rhs=wo_codes[:].bitcast(FP8X4),
                    rhs_scale=wo_scales[:],
                    start=True,
                    stop=True,
                )
            op[q, i] = acc

        def exit_out(q, i, engine):
            if q < 0 or i >= widths[q] // 256:
                return
            res = sb.tile([P, 2, H], F32, tag="ot", bufs=4, name="ot")
            bias = bo_t[:].unsqueeze(1).to_broadcast([P, 2, H])
            if engine == "v":
                nc.vector.tensor_tensor(out=res[:], in0=op[q, i][:], in1=bias, op=ADD)
            else:
                o_raw = sb.tile([P, 2, H], F32, tag="o_raw", bufs=3, name="o_raw")
                nc.scalar.copy(o_raw[:], op[q, i][:])
                nc.gpsimd.tensor_tensor(out=res[:], in0=o_raw[:], in1=bias, op=ADD)
            pair, j = starts[q] // PAIR, 2 * (starts[q] % PAIR // 256 + i)
            dst = out[PAIR * pair : PAIR * (pair + 1), :].rearrange("(p j) h -> p j h", j=4)
            nc.sync.dma_start(out=dst[:, j : j + 2, :], in_=res[:])

        w_raw, w_grp = {}, {}

        def load_w(m):
            t = raw.tile([P, 4, F], BF16, name="w_raw%d" % m)
            nc.sync.dma_start(out=t[:], in_=w[m].rearrange("(p j) f -> p j f", j=4))
            w_raw[m] = t

        def group_w(m, eng):
            t = raw.tile([P, F * 4], BF16, align_bytes=64, name="w_grp%d" % m)
            dst = t[:].rearrange("p (t c j) -> p t c j", t=4, j=4)
            src = w_raw[m][:].rearrange("p j (c t) -> p t c j", t=4)
            if eng == "v":
                nc.vector.tensor_copy(out=dst, in_=src)
            elif eng == "s":
                nc.scalar.copy(dst, src)
            else:
                for t4 in range(4):
                    nc.gpsimd.tensor_scalar(out=dst[:, t4], in0=src[:, t4], scalar1=1.0, scalar2=0.0, op0=MULT, op1=ADD)
            w_grp[m] = t

        def quant_w(m):
            nc.vector.quantize_mx(out=w_codes[:, m, :].bitcast(FP8X4), scales=w_scales[:, m, :], in_=w_grp[m][:])

        def load_wo():
            t = raw.tile([P, 4, H], BF16, name="wo_raw")
            nc.sync.dma_start(out=t[:], in_=wo.rearrange("(p j) h -> p j h", j=4))
            w_raw["o"] = t

        def group_wo():
            t = raw.tile([P, H * 4], BF16, align_bytes=64, name="wo_grp")
            nc.gpsimd.tensor_scalar(
                out=t[:].rearrange("p (h j) -> p h j", j=4),
                in0=w_raw["o"][:].rearrange("p j h -> p h j"),
                scalar1=1.0, scalar2=0.0, op0=MULT, op1=ADD,
            )
            w_grp["o"] = t

        def quant_wo():
            nc.vector.quantize_mx(out=wo_codes[:].bitcast(FP8X4), scales=wo_scales[:], in_=w_grp["o"][:])

        def constants():
            nc.vector.tensor_copy(out=b32[:], in_=b_raw[:])
            nc.vector.tensor_copy(out=om32[:], in_=om_raw[:])
            nc.vector.tensor_tensor(out=omb0[:], in0=om32[:], in1=b32[:, 0, :], op=MULT)

        def emit(item, s):
            kind = item[0]
            t = int(item[1]) if len(item) > 1 else 0
            if kind == "U":
                fuse(s - 1 - (t == 3), t)
            elif kind in "PR":
                if s >= 2 and t < widths[s - 2] // 256:
                    product(s - 2, CH * t, CH * (t + 1), "g" if kind == "P" else "v")
            elif kind == "M":
                project(s - 1, t, int(item[2]))
            elif kind == "A":
                exit0(s - 1, t)
            elif kind == "B":
                exit2(s - 1, t)
            elif kind == "O":
                project_out(s - 3, t)
            elif kind in "XY":
                exit_out(s - 3, t, "v" if kind == "X" else "s")
            elif kind == "C":
                cast(base[s] + 4 + t)
            elif kind == "E":
                rescale(base[s] + t)
            elif kind == "Z":
                rescale_s(base[s] + t)
            elif kind in "IJ":
                group_x(base[s] + t, "g" if kind == "J" else "s")
            elif kind in "TG":
                transpose(base[s] + 2 + t, kind == "G")
            elif kind == "D":
                pass
            elif kind == "W":
                group_w(t, "s")
            elif kind == "V":
                if t == 3:
                    quant_wo()
                else:
                    quant_w(t)
            elif kind == "K":
                constants()
            else:
                quant(s, 0, 12 * widths[s] + (4 * widths[s - 2] if s >= 2 else 0))

        with tc.manual_schedule():
            nc.vector.memset(warm[:], 0.0)
            load_x_half(0, 0)
            load_x_half(0, 1)
            load_w(0)
            load_x(0, 1)
            load_w(1)
            load_x(0, 2)
            load_w(2)
            load_wo()
            for m in range(MODS):
                load_x(1, m)
            nc.sync.dma_start(out=bo_t[:], in_=bo.partition_broadcast(P))
            nc.scalar.dma_start(out=scale[:], in_=x_scale.rearrange("o a (p t) -> p (o a t)", t=4))
            nc.scalar.activation(out=warm[:], in_=warm[:], func=IDENT)
            nc.scalar.dma_start(out=b_raw[:], in_=b.rearrange("m (p t) -> p m t", t=4))
            nc.scalar.dma_start(out=om_raw[:], in_=omega.rearrange("o (p t) -> p (o t)", t=4))
            make_identity(nc, ident[:])
            warm_ps = ps.tile([P, 512], F32, tag="tr", bufs=TRB, name="warm_ps")
            for k in range(HDUM):
                nc.tensor.matmul(warm_ps[:, 0:DN], lhsT=ident[:], rhs=ident[:, 0:DN], start=True, stop=True)
            for unit in range(4):
                cast(unit)
            transpose(0)
            transpose(1)
            group_w(0, "g")
            group_w(1, "g")
            group_wo()
            bodies = {"0": BODY0, "1": BODY, "2": BODY2, "7": BODY7, "8": BODY8, "T": BODYT}
            for s in range(STEPS + 1):
                if s < STEPS and starts[s] % PAIR == 0 and starts[s] // PAIR + 2 < TOKENS // PAIR:
                    for m in range(MODS):
                        load_x(starts[s] // PAIR + 2, m)
                for item in bodies[PLAN[s]].split():
                    emit(item.replace("'", ""), s + item.count("'"))
